import numpy as np, ml_dtypes
CORES = [36,164,52,180,100,228,116,244]
N = 8
BF = ml_dtypes.bfloat16
def gentries(a):
    return np.ascontiguousarray(a.reshape(8, 16, -1).transpose(0, 2, 1)).reshape(8, -1)
def gtable(e):
    e = np.asarray(e); return np.ascontiguousarray(e.reshape(8, -1, 16).transpose(0, 2, 1)).reshape(128, -1).astype(np.int32)
W, K, Q, ST, EV = 2048, 192, 2, 6, 3
def parts(rng):
    return {"turn": np.argsort(rng.random((8, W)), axis=1), "tw": rng.integers(0, 256, (8, 16, W)), "img": rng.integers(0, W, (N, 8, K, 16)),
            "ent": rng.integers(0, W, (N, 8, Q, W)), "elen": rng.integers(0, 25, (N, 8, W)), "own": rng.integers(0, W, (N, 8, Q, K)), "olen": rng.integers(0, 25, (N, 8, K))}
def flock(rng, img, share):
    c = np.where(rng.random((N, 8, K)) < share, rng.integers(0, K, (N, 8, K)), np.arange(K))
    o = np.argsort(rng.random(img.shape), axis=3)
    return np.take_along_axis(np.take_along_axis(img, c[..., None], 2), o, 3)
def pack(p):
    return {"turn": np.tile(p["turn"][None], (N, 1, 1)).astype(np.int32), "twist": np.tile(p["tw"].reshape(1, 128, W), (N, 1, 1)).astype(np.float32).astype(BF),
            "img": np.stack([gtable(a.reshape(8, 16 * K)) for a in p["img"]]), "ent": p["ent"].reshape(N, 8, Q * W).astype(np.int32), "elen": p["elen"].astype(np.int32),
            "own": p["own"].reshape(N, 8, Q * K).astype(np.int32), "olen": p["olen"].astype(np.int32)}
def setup_inputs(rng):
    p = parts(rng); p["img"] = flock(rng, p["img"], 0.4)
    return pack(p)
def setup_inputs_crowd(rng):
    p = parts(rng); base = rng.integers(0, W, (N, 8, 3, 16)); c = rng.integers(0, 3, (N, 8, K)); c[:, ::2] = 0
    p["img"] = np.take_along_axis(base, c[..., None], 2)
    p["olen"] = 5 + rng.integers(0, 2, (N, 8, K)) * rng.integers(0, 2, (N, 8, 1)); p["elen"] = rng.integers(0, 60, (N, 8, W))
    x = np.arange(W); j = np.arange(K)
    p["elen"][:, 2::2] = rng.integers(2000, 4096, (N, 3, W))
    p["olen"][:, 2] = 3 * (K - 1 - j) + int(rng.integers(0, 100)); p["olen"][:, 6] = 3 * j + int(rng.integers(0, 100))
    two = np.argsort(rng.random((N, W)), axis=1)[:, :8 * K].reshape(N, K // 2, 16)
    p["img"][:, 4] = two[:, rng.permutation(K) % (K // 2)]; p["olen"][:, 4] = rng.integers(0, 4, (N, K))
    n = K // ST; hop = W // (ST * Q); odd = 2 * int(rng.integers(1, W // 2)) + 1; o = (x * odd + int(rng.integers(0, W))) % W
    p["turn"][5] = (x + hop * odd) % W
    s = rng.permutation(K); a = np.minimum(j // n, ST - 1)[s]; i = (j % n)[s]
    p["img"][:, 5] = np.repeat(o[(i - a * Q * hop) % W][:, None], 16, axis=1)
    p["olen"][:, 5] = 3000 - 400 * a + rng.integers(0, 200, (N, K))
    p["elen"][:, 5] = 0; p["elen"][:, 5, o[:n]] = rng.integers(3500, 4096, (N, n))
    return pack(p)
def setup_inputs_ends(rng):
    p = parts(rng); v = np.array([0, 1, W // 2, W - 1]); e = np.array([0, 1, 4094, 4095]); x = np.arange(W)
    p["turn"][0] = x; p["turn"][1] = x[::-1]; p["turn"][2] = (x + 1) % W
    p["tw"][3] = 0; p["tw"][4] = 255 * rng.integers(0, 2, (16, W)); p["tw"][5] = 255
    p["img"][:, ::2] = rng.choice(v, (N, 4, K, 16)); p["img"][:, 1] = np.repeat(p["img"][:, 1, :, :1], 16, axis=2)
    p["ent"][:, 1:5] = rng.choice(v, (N, 4, Q, W)); p["own"][:, 1:5] = rng.choice(v, (N, 4, Q, K))
    p["elen"] = rng.choice(e, (N, 8, W)); p["olen"] = rng.choice(e, (N, 8, K)); p["olen"][int(rng.integers(0, N))] = 4095
    return pack(p)
def setup_inputs_full(rng):
    p = parts(rng); hop = W // (ST * Q); x = np.arange(W); j = np.arange(K)
    for g in range(8):
        c = int(rng.integers(1, W))
        if g < 4:
            o = (16 * np.argsort(rng.random((16, W // 16)), axis=1) + rng.permutation(16)[:, None]).reshape(W)
            p["ent"][:, g] = c; p["own"][:, g] = c
        else:
            o = (x * (2 * int(rng.integers(1, W // 2)) + 1) + int(rng.integers(0, W))) % W
        sig = np.zeros(W, np.int64); sig[o] = o[(x + hop) % W]
        p["turn"][g, (x + c) % W] = (sig + c) % W
        n = K if g % 2 else min(2 * K, Q * hop); z = np.argsort(rng.random((N, n)), axis=1)
        pts = o[np.stack([z[:, :K], z[:, np.where(K + j < n, K + j, j)]], axis=2)]
        p["img"][:, g] = np.take_along_axis(pts, np.argsort(rng.random((N, K, 16)), axis=2) % 2, 2)
        p["elen"][:, g, o] = 100 * (np.minimum(x // (Q * hop), ST - 1) + 1) + rng.integers(0, 50, (N, W)); p["olen"][:, g] = rng.integers(0, 50, (N, K))
    return pack(p)
def setup_inputs_spread(rng):
    p = parts(rng)
    p["tw"] = np.minimum((np.exp2(8 * rng.random((8, 1, W))) * rng.random((8, 16, W))).astype(np.int64), 255)
    p["img"] = flock(rng, np.minimum((W * rng.random((N, 8, K, 16)) ** 3).astype(np.int64), W - 1), 0.3)
    p["ent"] = np.minimum((W * rng.random((N, 8, Q, W)) ** 2).astype(np.int64), W - 1)
    p["elen"] = np.minimum(np.exp2(12 * rng.random((N, 8, W))).astype(np.int64), 4095); p["olen"] = np.minimum(np.exp2(12 * rng.random((N, 8, K))).astype(np.int64) - 1, 4095)
    return pack(p)
def setup_inputs_ties(rng):
    p = parts(rng); o = np.argsort(rng.random((8, 16, W)), axis=1)
    p["tw"] = o % 2 * 128; p["tw"][1] = o[1]; p["tw"][5] = o[5]; p["tw"][3::4] = rng.integers(0, 4, (2, 16, W))
    p["img"] = flock(rng, p["img"], 0.7)
    low = rng.permutation(np.array([0, 0, 0, 252, 1020, 2048, 3000, 4088])).reshape(1, 8, 1)
    p["elen"] = low + rng.integers(3, 6, (N, 8, W)); p["olen"] = low + rng.integers(3, 6, (N, 8, K))
    return pack(p)
def check_inputs(d):
    bad = []
    for k, hi in (("turn", W - 1), ("img", W - 1), ("ent", W - 1), ("own", W - 1), ("elen", 4095), ("olen", 4095)):
        if np.min(d[k]) < 0 or np.max(d[k]) > hi: bad.append("range of " + k)
    t = np.asarray(d["twist"]).astype(np.float32)
    if not np.all((t >= 0) & (t <= 255) & (t == np.floor(t))): bad.append("twist: whole numbers from 0 to 255")
    if not np.all(t == t[:1]): bad.append("twist alike on all ranks")
    if not np.all(np.sort(d["turn"], axis=2) == np.arange(W)): bad.append("turn: permutations")
    if not np.all(d["turn"] == d["turn"][:1]): bad.append("turn alike on all ranks")
    return bad
def reference(turn, twist, img, ent, elen, own, olen):
    pt = turn.astype(np.int64); tw = twist.astype(np.float32).astype(np.int64).reshape(N, 8, 16, W)
    b = np.stack([gentries(a) for a in img]).astype(np.int64)
    f = np.take_along_axis(tw, b[:, :, None, :], 3)
    e = ent.astype(np.int64).reshape(N, 8, Q, W); l = elen.astype(np.int64); o = own.astype(np.int64).reshape(N, 8, Q, K); m = olen.astype(np.int64)
    ri = np.arange(N).reshape(N, 1, 1); gi = np.arange(8).reshape(1, 8, 1); big = 2 ** 40
    for step in range(1, ST + 1):
        d = np.argmax(np.add.reduce(f, axis=2).reshape(N, 8, K, 16), axis=3)
        w = np.take_along_axis(b.reshape(N, 8, K, 16), d[..., None], 3)[..., 0]
        a = np.take_along_axis(e, w[:, :, None, :], 3); al = np.take_along_axis(l, w, 2)
        for q in range(Q):
            s = np.repeat(a[:, :, q], 16, axis=2); u = (b + s) & (W - 1)
            f = (f + np.take_along_axis(tw, u[:, :, None, :], 3)) & 255
            b = (np.take_along_axis(pt, u, 2) - s) & (W - 1)
        key = np.where(m < al, m * K + np.arange(K), big); best = np.full((N, 8, W), big)
        np.minimum.at(best, (ri, gi, w), key)
        won = (m < al) & (key == np.take_along_axis(best, w, 2))
        r1, g1, j1 = np.nonzero(won); x1 = w[r1, g1, j1]
        e[r1, g1, :, x1] = o[r1, g1, :, j1]; l[r1, g1, x1] = m[r1, g1, j1]
        m = np.where(won, al, m) + Q; o = a
        if step % EV == 0: e = np.roll(e, 1, axis=0); l = np.roll(l, 1, axis=0)
    return {"yimg": np.ascontiguousarray(b.reshape(N, 8, K, 16).transpose(0, 1, 3, 2)).reshape(N, 128, K).astype(np.float32), "yf": f.reshape(N, 128, 16 * K).astype(np.float32).astype(BF),
            "yent": e.reshape(N, 8, Q * W).astype(np.float32), "yelen": l.astype(np.float32)}

@@ -1,0 +1,528 @@
+import numpy as np
+from concourse.mybir import AluOpType as A, AxisListType, ActivationFunctionType as AF
+
+NW, NK, NST, NEV = 2048, 192, 6, 3
+TBW = NW + NK
+F32, BF, F16, I32, U16 = "float32", "bfloat16", "float16", "int32", "uint16"
+NCC = 19
+SCRATCH = {}
+
+
+def _sb(dtype, **kw):
+    for k, n in kw.items():
+        SCRATCH[k] = ("sbuf", [128] + (n if isinstance(n, list) else [n]), dtype)
+
+
+_sb(BF, fb=3072, big=128, tw=NW, Wn=4 * NW, ga=3072, qq=3072, eq=256, junk=384, Ib=128, nIb=128, BigZ=144, Wq=8, W0=8, YT=128,
+    CO=128, oneb=512)
+_sb(F16, hh0=3072, hh1=3072, tnh=512, FLW=NW, b16=192, Am=192, E0=192, E1=192, FL=192, Rr=192, Lm=[12, 32], flag=48, m0=12, m1=12)
+_sb(BF, Ic=128, nIc=128, BO=128, Big1=144, BigL=144, Wh=16, S0=128, S10=128, nS0=128, BP=128, TN=512, npw=512, Dm=128, DW=128,
+    Dt=128, Sub=128, EX=2048, JC=192, Sel01=128, Sel11=128, onec=128, Fold=224)
+_sb(I32, tni=512, TB1=TBW, b32=192, bt=192, owi=192, o15i=8, o4i=4, CM1=384, RC1=384)
+_sb(U16, u0=192, u1=192, wO=12, off=12, o15=8, o4=4)
+_sb(F32, TB2=TBW, TB3=TBW, Z1c=192, Zb=256, Aa=256, Kk=256, Mx=256, wf=12, acc=12, t1=12, t2=12, t3=12, SRC=204, RD3=204,
+    RD6=204, RF1=384, CM2=384, RC2=384, I32=128, nI32=128, segm=128, tie=128, tier=128, pw=128, d0=128, d1=128, two=16, zer=16,
+    VR=32 * NCC, CC=32 * NCC, Jf=192, dum=12, dumr=12, yi=192, TH=48)
+for _b in ("F0", "F1", "F2", "F3", "F4", "F5", "P0", "P1"):
+    SCRATCH[_b] = ("psum", [128, 512], F32)
+NDS = 40
+SEMAPHORES = ["sV", "sS", "sP", "sG"] + ["d%d" % i for i in range(NDS)] + ["r%d" % i for i in range(6)] + ["l%d" % i for i in range(6)]
+HBM = {"turn": [8, NW], "twist": [128, NW], "img": [128, NK], "ent": [8, 2 * NW], "elen": [8, NW], "own": [8, 2 * NK],
+       "olen": [8, NK], "yimg": [128, NK], "yf": [128, 3072], "yent": [8, 2 * NW], "yelen": [8, NW]}
+s_ = np.s_
+PAR = {"gv": (5,), "iv": (), "zp": ((0, 96),), "tb": 1600, "gc": 11, "cons": (2, 4, 6), "fs": (), "nb": 3}
+ORDER = r"021[010=000K0A1\0[0Z0I1a0O0W0D0E0B0Y0F0X0G0@0R1H0J031F0H1]0S1Q0U0P1>1L1O1S0>1;1T2L1G1P0\1N0Q041=1R0V0<2N1`0T0N0M250C1A202O1c06182P1_1M1V051:2>2T2Q0L261?2M1^1U2X2S2B0c2Y0;070i0:091W16080k1C10272:0l0e141<2?171I211B2U1X1J2;0n1E151b2Z0g281K2[0j1@2V2R0a2C2<0f29222f2\0_2W2g1D0o2=110]2@122]1h2^1Y0d0^2c2h0h2A2D2i0`1k1i2I131Z2_0?0m2j2E2`1j2a0b2b232J1o192H2F352G1d2d2k2e2K2l362m2n1e322o3334303f3O3N373h3g3i3M4D38391f3:3j3?243n1m3l3o3P1n3k3m3B3;401l3144414245463Q3@3<43474:484;4<3R493=3S3T1g4=3X3E3A4@3F4>3U4A3C4?3>3Y3[4B3V4C3D4H3^4G3G3Z4E4F3H3W4I3I3J3L3`4J3_3K3\4P4N4Q3a4R3]4K4S4L4T3e4O4U4M4]4V4W4[3b4X4^4Y3c4k4_3d4`4a4\4b4l4h4c4i4d4j5^4e5`4m5_4f5a5D5b4n6<505E5d5f5h54514g5e5g584o5i554Z6?5F59566=52575<5:535l5G5>5c5;5m5=5n5H5j6>625N5k5?5o605C615R5I6364665O675J656:6P686;5V6R5P5@6S5K5A695B6Q5X6@5W5Q6T5L6A6U5S6B6F6G5Y5T5M6H6J6I6V5Z5[5]6W6X6[6C6Y6^6Z6`6m6D6a5\6b6\6c6K5U6n6j6d6E6]6k6l6e7Z6f6g7\6o6h7[7D7]8870757C7^7b7`7d72767c7a7h7e7f7E6i737i6_7g7j777l787F7k717m89807G797_7I748B7;7:8:7n7L827<7J817o867H7O84837B87857M7K8<6L8=7N7R6M8>6O6N7=8C8F7P7S8G8;7T7>8H7Q7U7?7@8?8I7V8@7Y7A8J7W8K8S7X8T8D8L8E8Q8P8M8U8N8O8V8R8a8W8A8X8^8`8_8Y9T8Z8b8[9V:28\9U9W9:8c9<9Z8d9\9[9^8f9]9`9_9X9a9b9d9c8n9f8g9;8j9e9=8h8e8k9>9@9?9g9h8l9H9j8o9i9k9D9Y8]929n8m939L90949l8i9o:0999m:19E:>:@:3:A:5:6959F:491:79A96979N:89M9G:?9I9B:<98:9:=9O9J:::;:B:C9S9K:D:L:M:N9P:E:F:O:G:H:P9Q:[:J9R:Q:K:R:\:X:Y:S;H:T:Z9C:U;f:V;J;1;I;K;L;3;P:];Q;2;g;N:^;R;V:c;O;4;S:_;W:`:I;X;T:d;U:W;Y:f;Z:e;\:a;[;^;5:b:i;7;6:g;];_:k;`;=;8:j:h;b:l;a;:;9;0;c;d;@;i;h;M<9;e<:;><;:m;;;?:n;j;B;k:o;A;<<<;l;C<=<0<1;G<D<><F<3<4;D<2<G;E<?<H<C<@<I;F<A<J<B<Q<E<K<T;m;n;o<R<L=K<5<U<M<N=M=i<S=L=N<O=S=Q=1=T<V=R=j=U<W=Y=V=W<Y=Z=[=0=O=_<^<Z=X<o<c=]<_=P=\=o<P<[=k=2<6<8=^<\=`<`=a=e=3<]<d<7=5=b=f=:=c=g=d=6=4=h<X<a<e<h=l=7=?=m<i=;=n<f>0=8=@=<==<j=A=><b=9<g=D<k<l=B=E=F>1=C<m>2<n=G>4>5>3=H=I=J"
+
+
+def _shape(name):
+    return SCRATCH[name][1] if name in SCRATCH else HBM[name]
+
+
+def _dt(name):
+    return SCRATCH[name][2] if name in SCRATCH else F32
+
+
+def _box(x):
+    name, idx = x[0], x[1]
+    sh = _shape(name)
+    idx = idx if isinstance(idx, tuple) else (idx,)
+    idx = list(idx) + [slice(None)] * (len(sh) - len(idx))
+    rs = [range(sh[d])[i] if isinstance(i, slice) else range(i, i + 1) for d, i in enumerate(idx)]
+    lo = hi = 0
+    n = 1
+    for d in range(1, len(sh)):
+        lo, hi, n = lo * sh[d] + rs[d][0], hi * sh[d] + rs[d][-1], n * len(rs[d])
+    return (name, frozenset(rs[0]), lo, hi, n)
+
+
+def ap(name, idx=slice(None)):
+    return (name, idx)
+
+
+def ind(win, offs):
+    return (win[0], win[1], offs)
+
+
+def build():
+    ops = []
+    tag = ["i", 0]
+
+    def add(eng, kind, args, reads, writes):
+        rd, wr = [], []
+        for x in reads:
+            if isinstance(x, tuple):
+                rd.append(_box(x))
+                if len(x) == 3:
+                    rd.append(_box(x[2]))
+        for x in writes:
+            wr.append(_box(x))
+            if len(x) == 3:
+                rd.append(_box(x[2]))
+        ops.append(dict(eng=eng, kind=kind, args=args, rd=rd, wr=wr, tag=tag[0], st=tag[1]))
+
+    def copy(out, in_):
+        add("V", "copy", (out, in_), [in_], [out])
+
+    def ts(out, in_, a, b, o0, o1=None):
+        add("V", "ts", (out, in_, a, b, o0, o1), [in_, a, b], [out])
+
+    def tt(out, x, y, o):
+        add("V", "tt", (out, x, y, o), [x, y], [out])
+
+    def mset(out, v):
+        add("V", "mset", (out, v), [], [out])
+
+    def scan(out, x, y, init, o0, o1):
+        add("V", "scan", (out, x, y, init, o0, o1), [x, y], [out])
+
+    def act(out, in_, func=AF.Identity, bias=0.0, scale=1.0, accum=None):
+        add("S", "act", (out, in_, func, bias, scale, accum), [in_, bias, scale], [out] + ([accum] if accum else []))
+
+    def scaled(out, in_, col):
+        act(out, in_, AF.Identity, 0.0, col)
+
+    def mm(lst):
+        add("P", "mm", lst, [x[1] for x in lst] + [x[2] for x in lst] + [x[0] for x in lst if not x[3]], [x[0] for x in lst])
+
+    def grp(items):
+        return [(o, l, r, k == 0, k == len(items) - 1) for k, (o, l, r) in enumerate(items)]
+
+    def iota(out, pat, base, cm):
+        add("G", "iota", (out, pat, base, cm), [], [out])
+
+    def asel(out, in_, pat, cmp, fill, base, cm):
+        add("G", "asel", (out, in_, pat, cmp, fill, base, cm), [in_], [out])
+
+    def dma(out, in_, q="Y"):
+        add(q, "dma", (out, in_), [in_], [out])
+
+    def remote(out, in_):
+        add("G", "rem", (out, in_), [in_], [out])
+
+    def cc(k):
+        return ap("CC", s_[:, 32 * k:32 * k + 1])
+
+    TROW = (0, 1, 11)
+
+    dma(ap("b32"), ap("img"))
+    dma(ap("tw", s_[:, 0:1024]), ap("twist", s_[:, 0:1024]))
+    dma(ap("tw", s_[:, 1024:2048]), ap("twist", s_[:, 1024:2048]), "S")
+    dma(ap("tni", s_[0:32, :]), ap("turn"), "S")
+    mset(ap("owi"), 0)
+    mset(ap("TB1", s_[:, PAR["tb"]:]), 0)
+    iota(ap("TB1", s_[:, 0:PAR["tb"]]), [[0, PAR["tb"]]], 0, 0)
+    for k, (src, osrc) in enumerate(((ap("ent", s_[:, 0:NW]), ap("own", s_[:, 0:NK])), (ap("ent", s_[:, NW:]), ap("own", s_[:, NK:])),
+                                     (ap("elen"), ap("olen")))):
+        dma(ap("TB1", s_[TROW[k]::16, 0:NW]), src)
+        dma(ap("owi", s_[TROW[k]::16, :]), osrc)
+
+    mset(ap("onec"), 1.0)
+    mset(ap("oneb", s_[0:32, :]), 1.0)
+    mset(ap("big", s_[0:32, :]), 49152.0)
+    asel(ap("Ic"), ap("onec"), [[-1, 128]], A.is_equal, 0.0, 0, 1)
+    asel(ap("BO"), ap("onec"), [[-16, 8], [0, 16]], A.is_ge, 0.0, 0, 1)
+    asel(ap("BO"), ap("BO"), [[16, 8], [0, 16]], A.is_ge, 0.0, 15, -1)
+    asel(ap("Sub"), ap("onec"), [[-1, 128]], A.is_equal, 0.0, -1, 1)
+    mset(ap("segm"), 1.0)
+    mset(ap("segm", s_[:, 0::16]), 0.0)
+    act(ap("d0"), ap("segm"), AF.Identity, 0.0, 0.5)
+    ts(ap("d1"), ap("segm"), -1.0, 1.0, A.mult, A.add)
+    scan(ap("pw"), ap("d0"), ap("d1"), 0.0, A.mult, A.add)
+    mset(ap("two"), 2.0)
+    mset(ap("zer"), 0.0)
+    mset(ap("VR", s_[:, 0:320]), 0.0)
+    mset(ap("VR", s_[:, 320:]), 0.0)
+
+    def vr(k, t0, t1, v, go=None):
+        if go is None and t1 - t0 == 1:
+            parts = [ap("VR", s_[:, 32 * k + t0:32 * k + 32:16])]
+        else:
+            parts = [ap("VR", s_[:, 32 * k + 16 * o + t0:32 * k + 16 * o + t1]) for o in ((0, 1) if go is None else (go,))]
+        for x in parts:
+            if k >= PAR["gc"]:
+                iota(x, [[0, _box(x)[4]]], int(v), 0)
+            else:
+                mset(x, v)
+    for o in (0, 1):
+        scan(ap("VR", s_[:, 16 * o:16 * o + 11]), ap("two", s_[:, 0:11]), ap("zer", s_[:, 0:11]), 2.0 ** -9, A.mult, A.add)
+    vr(1, 0, 1, 1.0); vr(2, 0, 1, -1.0); vr(2, 1, 2, 1.0); vr(3, 11, 12, 1.0); vr(4, 11, 12, -2048.0); vr(5, 11, 12, 2048.0)
+    vr(6, 0, 11, 1.0); vr(7, 1, 12, -2.0); vr(8, 0, 2, 1.0); vr(9, 12, 13, 1.0 / 256); vr(9, 14, 15, 1.0 / 256)
+    ts(ap("VR", s_[:, 320:352]), ap("pw", s_[:, 0:32]), 0.5, 1023.5, A.mult, A.add)
+    vr(10, 0, 1, 0.0); vr(18, 1, 32, 1024.0, 0); vr(18, 0, 1, 0.0, 1)
+    vr(11, 0, 11, 128.0); vr(11, 11, 13, 1.0)
+    vr(12, 0, 1, 128.0 * 2048 - 64); vr(12, 1, 11, 128.0 * 1024 - 64); vr(12, 13, 15, 1.0); vr(12, 15, 16, 64.0)
+    for o in (0, 1):
+        vr(13 + 2 * o, 0, 11, -64.0, o); vr(13 + 2 * o, 13, 15, -1.0, o)
+        vr(14 + 2 * o, 0, 1, 32 - 64.0 * 2048, o); vr(14 + 2 * o, 1, 11, 32 - 64.0 * 1024, o)
+        vr(14 + 2 * o, 11, 13, 1.0, o); vr(14 + 2 * o, 15, 16, 352.0, o)
+    iota(ap("VR", s_[:, 544:576]), [[0, 2], [1, 16]], 0, 0)
+    add("V", "vtr", (ap("CC", s_[:, 0:320]), ap("VR", s_[:, 0:320])), [ap("VR", s_[:, 0:320])], [ap("CC", s_[:, 0:320])])
+    add("V", "vtr", (ap("CC", s_[:, 320:]), ap("VR", s_[:, 320:])), [ap("VR", s_[:, 320:])], [ap("CC", s_[:, 320:])])
+    BM = ap("BO", s_[:, 0::16])
+    scaled(ap("Ib"), ap("Ic"), 1.0); scaled(ap("nIb"), ap("Ic"), -1.0); scaled(ap("nIc"), ap("Ic"), -1.0)
+    scaled(ap("I32"), ap("Ic"), 1.0); scaled(ap("nI32"), ap("Ic"), -1.0)
+    for nm, col in (("BigZ", cc(0)), ("Big1", 1.0), ("BigL", cc(3))):
+        mset(ap(nm), 0.0)
+        scaled(ap(nm, s_[:, 15:143:16]), BM, col)
+    scaled(ap("Wh", s_[:, 0:8]), BM, cc(0)); scaled(ap("Wh", s_[:, 8:16]), BM, 1.0)
+    scaled(ap("Wq"), BM, -1.0); scaled(ap("W0"), BM, 1.0)
+    scaled(ap("S0"), ap("BO"), cc(1)); scaled(ap("S10"), ap("BO"), cc(2)); scaled(ap("nS0"), ap("S0"), -1.0)
+    tt(ap("BP"), ap("BO"), ap("pw"), A.mult)
+    scaled(ap("YT"), ap("BP"), cc(0))
+    for k in range(4):
+        scaled(ap("npw", s_[0:32, 128 * k:128 * k + 128]), ap("pw", s_[0:32, :]), -1.0)
+    asel(ap("TN", s_[0:32, :]), ap("npw", s_[0:32, :]), [[-1, 4], [-4, 8], [0, 16]], A.is_equal, 0.0, 0, 1)
+    scaled(ap("CO", s_[0:32, :]), ap("pw", s_[0:32, :]), 2.0 ** -9)
+    asel(ap("CO", s_[0:32, :]), ap("CO", s_[0:32, :]), [[0, 128]], A.is_equal, -0.5, -1, 1)
+    scaled(ap("Dt"), ap("Sub"), cc(7)); scaled(ap("Dm"), ap("Ic"), cc(6))
+    tt(ap("Dm"), ap("Dm"), ap("Dt"), A.add)
+    scaled(ap("DW"), ap("Dm"), -256.0)
+    scaled(ap("Sel01"), ap("Ic"), cc(8)); scaled(ap("Sel11"), ap("Ic"), cc(3))
+    iota(ap("tier"), [[0, 8], [-1, 16]], 16, 0)
+    scaled(ap("tie"), ap("tier"), 1.0 / 16)
+    iota(ap("o15i"), [[16, 8]], 15, 0)
+    copy(ap("o15"), ap("o15i"))
+    mset(ap("Kk", s_[96:128, :]), 0.0); mset(ap("Mx", s_[96:128, :]), 0.0)
+    iota(ap("Jf"), [[1, NK]], 0, 0)
+    scaled(ap("JC"), ap("Jf"), cc(9))
+    iota(ap("dumr"), [[16, 12]], NW, 0)
+    ts(ap("dum"), ap("dumr"), cc(17), None, A.add)
+    copy(ap("o4i"), ap("dum", s_[:, 0:4]))
+    ts(ap("o4i"), ap("o4i"), 2, 511, A.logical_shift_right, A.bitwise_and)
+    copy(ap("o4"), ap("o4i"))
+    iota(ap("TH"), [[0, 48]], 0, 0)
+    asel(ap("TH"), ap("TH"), [[0, 12], [-32, 4]], A.is_ge, 1e9, 0, 1)
+    asel(ap("TH"), ap("TH"), [[0, 12], [32, 4]], A.is_ge, 1e9, 31, -1)
+    mset(ap("Fold"), 0.0)
+    for x in range(4):
+        scaled(ap("Fold", s_[32 * x:32 * x + 32, 96:128]), ap("Ic", s_[32 * x:32 * x + 32, 32 * x:32 * x + 32]), 8192.0)
+    mset(ap("EX"), 0.0)
+    for t in (11, 13):
+        asel(ap("EX", s_[:, t::16]), ap("onec"), [[-1, 16], [-16, 8]], A.is_equal, 0.0, 0, 1)
+    iota(ap("TB2"), [[0, TBW]], 0, 0)
+    iota(ap("TB3"), [[0, TBW]], 0, 0)
+
+    copy(ap("tnh", s_[0:32, :]), ap("tni", s_[0:32, :]))
+    MAG = 1.5 * 2 ** 23
+    for k in range(4):
+        cs = s_[:, 512 * k:512 * k + 512]
+        yb = ap("F%d" % k)
+        mm(grp([(yb, ap("YT"), ap("tw", cs)), (yb, ap("TN", s_[0:32, 128 * k:128 * k + 128]), ap("tnh", s_[0:32, :])),
+                (yb, ap("CO", s_[0:2, :]), ap("oneb", s_[0:2, :]))]))
+        ts(ap("FLW", cs), yb, MAG, MAG, A.add, A.subtract)
+        wb = ap("F%d" % (4 + k % 2))
+        mm(grp([(wb, ap("Ib"), ap("tw", cs)), (wb, ap("DW"), ap("FLW", cs))]))
+        act(ap("Wn", cs), wb)
+    for k in (1, 2, 3):
+        dma(ap("Wn", s_[:, k * NW:(k + 1) * NW]), ap("Wn", s_[:, 0:NW]))
+
+    def ln(name, c):
+        return ap(name, s_[:, 96 * c:96 * c + 96])
+
+    def lm(name, c, p=96):
+        return ap(name, s_[0:p, 128 * c:128 * c + 128])
+
+    def pb(c, a, b, p=128, st=None):
+        return ap("P%d" % c, s_[0:p, a:b:st])
+
+    def qb(c, a, b, p=128, st=None):
+        return ap("F%d" % (PAR["nb"] + c), s_[0:p, a:b:st])
+
+    def im(name, c, i):
+        return ap(name, s_[:, 1536 * c + i:1536 * c + 1536:16])
+
+    def diag(big, rhs, out):
+        return [(out, ap(big, s_[:, 15 - k:143 - k]), rhs(k)) for k in range(16)]
+
+    ts(ap("E0"), ap("owi"), cc(4), None, A.add)
+    mm(grp(diag("BigL", lambda k: ap("E0", s_[:, k::16]), pb(1, 448, 460))))
+    copy(ap("m0"), pb(1, 448, 460))
+    copy(ap("u1"), ap("b32"))
+    copy(ap("b16"), ap("b32"))
+    for c in range(2):
+        for p in range(2):
+            (copy if 2 * c + p in PAR["iv"] else act)(ap("fb", s_[:, 1536 * c + 768 * p:1536 * c + 768 * p + 768]),
+                                                      ind(ap("tw"), ap("u1", s_[:, 96 * c + 48 * p:96 * c + 48 * p + 48])))
+        mm([(pb(c, i, 128, 96, 16), im("fb", c, i), ap("W0"), True, True) for i in range(16)])
+        tt(lm("Kk", c), pb(c, 0, 128, 96), ap("tie", s_[0:96, :]), A.add)
+        act(lm("Aa", c), lm("Kk", c), AF.Identity, 16 * 49152.0)
+    held = []
+
+    OFF = 4096 - 127.5 / 256
+    for st in range(1, NST + 1):
+        tag[1] = st
+        hh = "hh%d" % len(held)
+        held.append(hh)
+        cons = st in PAR["cons"]
+        TB = "TB1" if st <= NEV else "TB2"
+        En, Ep = "E%d" % (st % 2), "E%d" % (1 - st % 2)
+        mo, mn = "m%d" % (1 - st % 2), "m%d" % (st % 2)
+        for c in range(2):
+            tag[0] = "a%d" % c
+            if st > 1:
+                tt(lm("Kk", c), pb(c, 0, 128, 96), lm("Aa", c), A.add)
+                if st - 1 in PAR["cons"] and st < NST:
+                    act(lm("Aa", c), lm("Kk", c), AF.Identity, 16 * 49152.0)
+            scan(lm("Mx", c), ap("segm", s_[0:96, :]), lm("Kk", c), 0.0, A.mult, A.max)
+            tt(lm("eq", c, 128), ind(lm("Mx", c, 128), ap("o15")), lm("Kk", c, 128), A.is_equal)
+            mm([(pb(c, 0, 96), lm("eq", c), ap("Ib", s_[0:96, 0:96]), True, True)])
+            tt(ln("Am", c), pb(c, 0, 96), ln("b16", c), A.mult)
+            mm(grp(diag("Big1", lambda k: ap("Am", s_[:, 96 * c + k:96 * c + 96:16]), pb(c, 224, 230))))
+            wo = ap("wO", s_[:, 6 * c:6 * c + 6])
+            copy(wo, pb(c, 224, 230))
+            ts(ln(En, c), ind(ap(TB), wo), cc(4), None, A.add)
+            mm(grp([(pb(c, 0, 96), ap("Ic"), ln("b16", c)), (pb(c, 0, 96), ap("S0"), ln(En, c))]))
+            if st > 1:
+                copy(ln("u0", c), pb(c, 0, 96))
+            else:
+                copy(ln("bt", c), pb(c, 0, 96))
+                ts(ln("bt", c), ln("bt", c), NW - 1, None, A.bitwise_and)
+                copy(ln("u0", c), ln("bt", c))
+            act(ap("wf", s_[:, 6 * c:6 * c + 6]), pb(c, 224, 230))
+            mm([(pb(c, 128, 224), ap("BP"), ln("Am", c), True, True)])
+            ts(ln("FL", c), pb(c, 128, 224), cc(10), cc(18), A.add, A.max)
+        for c in range(2):
+            tag[0] = "b%d" % c
+            for k in range(3 * c, 3 * c + 3):
+                (copy if k in PAR["gv"] else act)(ap("ga", s_[:, 512 * k:512 * k + 512]),
+                                                  ind(ap("Wn", s_[:, 0:2 * NW if st > 1 else NW]), ap("u0", s_[:, 32 * k:32 * k + 32])))
+            for (l0, l1) in PAR["zp"]:
+                z, cl = pb(c, l0, l1), s_[:, 96 * c + l0:96 * c + l1]
+                mm(grp(diag("BigZ", lambda i: ap("ga", s_[:, 1536 * c + 16 * l0 + i:1536 * c + 16 * l1:16]), z) + [(z, ap("S10"), ap(En, cl))]))
+                if st > 1:
+                    ts(ap("u1", cl), z, OFF, None, A.add)
+                else:
+                    ts(ap("bt", cl), z, OFF, None, A.add)
+                    ts(ap("bt", cl), ap("bt", cl), NW - 1, None, A.bitwise_and)
+                    copy(ap("u1", cl), ap("bt", cl))
+            act(ln("Z1c", c), pb(c, 0, 96))
+            for k in range(3 * c, 3 * c + 3):
+                cs = s_[:, 512 * k:512 * k + 512]
+                fb = ap("F%d" % (k % PAR["nb"]))
+                tt(ap(hh, cs), ind(ap("Wn", s_[:, 0:4 * NW if st > 1 else NW]), ap("u1", s_[:, 32 * k:32 * k + 32])), ap("ga", cs), A.add)
+                twice = cons and (st, k) in PAR["fs"]
+                terms = [(fb, ap("Ib"), ap("fb", cs))] + [(fb, ap("Ic"), ap(x, cs)) for x in held]
+                mm(grp(terms + ([(fb, ap("big", s_[0:1, :]), ap("oneb", s_[0:1, :]))] if cons and not twice else [])))
+                act(ap("qq", cs), fb, AF.Identity, -127.5 if cons and not twice else 49024.5)
+                if twice:
+                    mm(grp(terms + [(fb, ap("nIb"), ap("qq", cs))]))
+                    act(ap("fb", cs), fb, AF.Identity, 49152.0)
+                elif cons:
+                    tt(ap("fb", cs), fb, ap("qq", cs), A.subtract)
+                if st == NST:
+                    dma(ap("yf", cs), ap("fb", cs))
+            nf = 8 if st == NST else 16
+            mm([(pb(c, i, 16 * nf, 96, 16), im(hh, c, i), ap("Wh", s_[:, 0:nf]), True, True) for i in range(16)])
+            act(lm("Zb", c), pb(c, 0, 128, 96))
+            if st < NST:
+                tt(lm("Aa", c), pb(c, 128, 256, 96), lm("Aa", c), A.add)
+            mm(grp([(pb(c, 128, 224), lm("Zb", c), ap("I32", s_[0:96, 0:96])), (pb(c, 128, 224), ap("nI32"), ln("Z1c", c)),
+                    (pb(c, 128, 224), ap("nS0"), ln(En, c))]))
+            ts(ln("bt", c), pb(c, 128, 224), OFF, None, A.add)
+            ts(ln("b32", c), ln("bt", c), NW - 1, None, A.bitwise_and)
+            if st < NST:
+                copy(ln("b16", c), ln("b32", c))
+                mm([(pb(c, i, 128, 96, 16), im("qq", c, i), ap("Wq"), True, True) for i in range(16)])
+            else:
+                copy(ln("yi", c), ln("b32", c))
+                dma(ln("yimg", c), ln("yi", c))
+        tag[0] = "c"
+        if cons:
+            held = []
+        X = qb(0, 256, 448)
+        mm([(X, ap("Dm"), ap("FL"), True, False), (X, ap("Ic"), ap("JC"), False, False)]
+           + [(qb(0, 256 + k, 448, 128, 16), ap("EX", s_[:, 128 * k:128 * k + 128]), ap(mo), False, k == 15) for k in range(16)])
+        ts(ap("Rr"), X, cc(11), cc(12), A.mult, A.add)
+        for o in (0, 1):
+            ts(ap("Lm", s_[:, :, 16 * o:16 * o + 16]), X, cc(13 + 2 * o), cc(14 + 2 * o), A.mult, A.add)
+        mm(grp([(qb(1, 256, 448), ap("Sel01"), ap(Ep)), (qb(1, 256, 448), ap("Sel11"), ap("Rr"))]))
+        act(ap("SRC", s_[:, 0:NK]), qb(1, 256, 448), AF.Identity, cc(5))
+        for k in range(12):
+            a, cb = k // 3, k % 3
+            D = qb(k % 3, 0, 192)
+            mm([(D, ap("Lm", s_[32 * a:32 * a + 32, 4 * cb:4 * cb + 4, :]), ap("Rr", s_[32 * a:32 * a + 32, :]), True, True)])
+            act(ap("junk", s_[:, 192 * (k % 2):192 * (k % 2) + 192]), D, AF.Relu, 0.0, -1.0, ap("acc", s_[:, k:k + 1]))
+        Y = qb(1, 448, 460)
+        mm(grp(diag("BigL", lambda k: ap(En, s_[:, k::16]), Y) + [(Y, ap("nIc"), ap(mo))]))
+        ts(ap("t1"), Y, 0.0, 8192.0, A.is_le, A.mult)
+        tt(ap("t1"), ap("t1"), ap("wf"), A.add)
+        if st < NST:
+            tt(ap("t2"), Y, ap("wf"), A.add)
+        tt(ap("flag"), ind(ap("acc"), ap("o4", s_[:, 0:3])), ap("TH"), A.is_gt)
+        Y = qb(1, 464, 476)
+        mm(grp([(Y, ap("I32"), ap("t1"))]
+               + [(Y, ap("Fold", s_[:, 96 - 32 * a:224 - 32 * a]), ap("flag", s_[:, 12 * a:12 * a + 12])) for a in range(4)]))
+        tt(ap("SRC", s_[:, NK:]), Y, ap("dum"), A.min)
+        if st < NST:
+            tt(ap("t3"), ap("t2"), Y, A.subtract)
+            ts(ap("t3"), ap("t3"), 0.0, 2.0, A.max, A.add)
+            tt(ap(mn), ap("t3"), ap(mo), A.add)
+        src, tb = "SRC", TB
+        if st % NEV == 0:
+            src, tb = "RD%d" % st, ("TB2" if st == NEV else "TB3")
+            remote(ap(src, s_[:, 0:NK]), ap("SRC", s_[:, 0:NK]))
+            remote(ap(src, s_[:, NK:]), ap("SRC", s_[:, NK:]))
+        copy(ap("off"), ap(src, s_[:, NK:]))
+        copy(ind(ap(tb), ap("off")), ap(src, s_[:, 0:NK]))
+        if st % NEV == NEV - 1:
+            cm, rc, nb = ("CM1", "RC1", "TB2") if st < NEV else ("CM2", "RC2", "TB3")
+            for k in range(3):
+                dma(ap(cm, s_[:, 128 * k:128 * k + 128]), ap(TB, s_[TROW[k]::16, 0:NW]))
+            remote(ap(rc), ap(cm))
+            if st < NEV:
+                copy(ap("RF1"), ap(rc))
+                rc = "RF1"
+            for k in range(3):
+                dma(ap(nb, s_[TROW[k]::16, 0:NW]), ap(rc, s_[:, 128 * k:128 * k + 128]))
+    for k, o in enumerate((ap("yent", s_[:, 0:NW]), ap("yent", s_[:, NW:]), ap("yelen"))):
+        dma(o, ap("TB3", s_[TROW[k]::16, 0:NW]))
+    return ops
+
+
+def link(ops):
+    hist = {}
+    for i, o in enumerate(ops):
+        d = {}
+        for mine, lst in ((False, o["rd"]), (True, o["wr"])):
+            for bx in lst:
+                for (j, w, b2) in hist.get(bx[0], []):
+                    if (w or mine) and bx[2] <= b2[3] and b2[2] <= bx[3] and not bx[1].isdisjoint(b2[1]):
+                        d[j] = d.get(j, False) or w
+        o["dep"] = d
+        o["banks"] = sorted(set(b[0] for b in o["rd"] + o["wr"] if b[0] in SCRATCH and SCRATCH[b[0]][0] == "psum"))
+        for w, lst in ((False, o["rd"]), (True, o["wr"])):
+            for bx in lst:
+                hist.setdefault(bx[0], []).append((i, w, bx))
+
+
+def plan():
+    ops = build()
+    link(ops)
+    order = [(ord(ORDER[2 * k]) - 48) * 64 + ord(ORDER[2 * k + 1]) - 48 for k in range(len(ORDER) // 2)]
+    cnt, nd, nr, bank = {}, 0, 0, {}
+    for i in order:
+        o = ops[i]
+        for b in o["banks"]:
+            for e, j in bank.setdefault(b, {}).items():
+                if e != o["eng"]:
+                    o["dep"][j] = True
+            bank[b][o["eng"]] = i
+        if o["kind"] == "dma":
+            o["sig"] = ("d%d" % nd, 16)
+            nd += 1
+        elif o["kind"] == "rem":
+            o["sig"] = nr
+            nr += 1
+        else:
+            cnt[o["eng"]] = cnt.get(o["eng"], 0) + 1
+            o["sig"] = ("s" + o["eng"], cnt[o["eng"]])
+    return ops, order, cnt, nd, nr
+
+
+_PLAN = []
+
+
+def rank_program(g, core, T, topo):
+    rank = T.rank_of(core)
+    if rank is None:
+        return
+    if not _PLAN:
+        _PLAN.append(plan())
+    ops, order, cnt, nd, nr = _PLAN[0]
+    nxt = T.cores[(rank + 1) % len(T.cores)]
+    prv = T.cores[(rank - 1) % len(T.cores)]
+    rid, pid = topo.addr(nxt, core)
+    mask = topo.mask(core, nxt)
+    n_out, n_in = len(topo.engines(core, nxt)), len(topo.engines(prv, core))
+    Q = {"V": g.vector, "S": g.scalar, "P": g.tensor, "G": g, "Y": g.sync}
+
+    def r(x):
+        if not isinstance(x, tuple):
+            return x
+        v = T[x[0]][x[1]]
+        return v.indirect(r(x[2])) if len(x) == 3 else v
+
+    seen = {}
+
+    def wait(e, sem, val):
+        if seen.get((e, sem), 0) < val:
+            seen[(e, sem)] = val
+            Q[e].wait_ge(T.sem[sem], val)
+
+    for i in order:
+        o = ops[i]
+        e, k, a = o["eng"], o["kind"], o["args"]
+        need = {}
+        for j, w in o["dep"].items():
+            p = ops[j]
+            if p["kind"] == "rem":
+                sem, val = ("r%d" % p["sig"], n_in) if w else ("l%d" % p["sig"], n_out)
+            else:
+                sem, val = p["sig"]
+            if e == "P" and sem == "sP":
+                continue
+            need[sem] = max(need.get(sem, 0), val)
+        for sem in sorted(need):
+            wait(e, sem, need[sem])
+        q = Q[e]
+        if k == "rem":
+            g.remote_dma(r(a[0]), r(a[1]), T.sem["r%d" % o["sig"]], T.sem["l%d" % o["sig"]], pid, rid, mask)
+            continue
+        if k == "copy":
+            x = q.tensor_copy(r(a[0]), r(a[1]))
+        elif k == "ts":
+            x = (q.tensor_scalar(r(a[0]), r(a[1]), r(a[2]), None, a[4]) if a[5] is None
+                 else q.tensor_scalar(r(a[0]), r(a[1]), r(a[2]), r(a[3]), a[4], a[5]))
+        elif k == "tt":
+            x = q.tensor_tensor(r(a[0]), r(a[1]), r(a[2]), a[3])
+        elif k == "mset":
+            x = q.memset(r(a[0]), a[1])
+        elif k == "scan":
+            x = q.tensor_tensor_scan(r(a[0]), r(a[1]), r(a[2]), a[3], a[4], a[5])
+        elif k == "vtr":
+            x = q.transpose(r(a[0]), r(a[1]))
+        elif k == "act":
+            if a[5] is None:
+                x = q.activation(r(a[0]), r(a[1]), a[2], bias=r(a[3]), scale=r(a[4]))
+            else:
+                x = q.activation(r(a[0]), r(a[1]), a[2], bias=r(a[3]), scale=r(a[4]), accum_out=r(a[5]))
+        elif k == "mm":
+            for (out, l, rh, s0, s1) in a:
+                x = q.matmul(r(out), r(l), r(rh), s0, s1)
+        elif k == "iota":
+            if _dt(a[0][0]) == I32:
+                x = q.iota(r(a[0]), a[1], a[2], a[3])
+            else:
+                x = q.iota(r(a[0]), a[1], a[2], a[3], allow_small_or_imprecise_dtypes=True)
+        elif k == "asel":
+            x = q.affine_select(r(a[0]), r(a[1]), a[2], a[3], a[4], a[5], a[6])
+        else:
+            x = q.dma_start(r(a[0]), r(a[1]))
+        x.then_inc(T.sem[o["sig"][0]], 16 if k == "dma" else 1)
+    for e in sorted(cnt):
+        wait("G", "s" + e, cnt[e])
+    for k in range(nd):
+        wait("G", "d%d" % k, 16)
+    for k in range(nr):
+        wait("G", "r%d" % k, n_in)
+        wait("G", "l%d" % k, n_out)

@@ -1,10 +1,10 @@
 import numpy as np
-from concourse.mybir import AluOpType as A, AxisListType, ActivationFunctionType as AF
+from concourse.mybir import AluOpType as A, ActivationFunctionType as AF
 
 NW, NK, NST, NEV = 2048, 192, 6, 3
 TBW = NW + NK
 F32, BF, F16, I32, U16 = "float32", "bfloat16", "float16", "int32", "uint16"
-NCC = 19
+NCC = 10
 SCRATCH = {}
 
 
@@ -13,25 +13,33 @@ def _sb(dtype, **kw):
         SCRATCH[k] = ("sbuf", [128] + (n if isinstance(n, list) else [n]), dtype)
 
 
-_sb(BF, fb=3072, big=128, tw=NW, Wn=4 * NW, ga=3072, qq=3072, eq=256, junk=384, Ib=128, nIb=128, BigZ=144, Wq=8, W0=8, YT=128,
-    CO=128, oneb=512)
-_sb(F16, hh0=3072, hh1=3072, tnh=512, FLW=NW, b16=192, Am=192, E0=192, E1=192, FL=192, Rr=192, Lm=[12, 32], flag=48, m0=12, m1=12)
-_sb(BF, Ic=128, nIc=128, BO=128, Big1=144, BigL=144, Wh=16, S0=128, S10=128, nS0=128, BP=128, TN=512, npw=512, Dm=128, DW=128,
-    Dt=128, Sub=128, EX=2048, JC=192, Sel01=128, Sel11=128, onec=128, Fold=224)
-_sb(I32, tni=512, TB1=TBW, b32=192, bt=192, owi=192, o15i=8, o4i=4, CM1=384, RC1=384)
-_sb(U16, u0=192, u1=192, wO=12, off=12, o15=8, o4=4)
-_sb(F32, TB2=TBW, TB3=TBW, Z1c=192, Zb=256, Aa=256, Kk=256, Mx=256, wf=12, acc=12, t1=12, t2=12, t3=12, SRC=204, RD3=204,
-    RD6=204, RF1=384, CM2=384, RC2=384, I32=128, nI32=128, segm=128, tie=128, tier=128, pw=128, d0=128, d1=128, two=16, zer=16,
-    VR=32 * NCC, CC=32 * NCC, Jf=192, dum=12, dumr=12, yi=192, TH=48)
-for _b in ("F0", "F1", "F2", "F3", "F4", "F5", "P0", "P1"):
+_sb(BF, tw=NW, Wn=4 * NW, qq=3072, fo=3072, junk=400, ge=288, nI1=96, flag=12, onec=128, zerc=128, Ib=128, nIb=128, BO=128, BigZ=144,
+    Big1=144, Wh=16, Wq=8, S0=128, S10=128, nS0=128, nS1=128, BP=128, YT=128, TN=512, npw=128, DW=[8, 16], SelL=128, SelM=128,
+    Sel01=128, Sel11=128, SelJ=128, JC=NK, neg2=NK, mid=NK, Fold=128, high=128, ones=512)
+_sb(F16, X=3072, Y=3072, FD=3072, tnh=512, FLW=NW, b16=NK, Am=NK, E0=NK, E1=NK, FL=NK, mf=NK, Rr=194, Lm=[12, 32], wf=12)
+_sb(I32, tni=512, b32=NK, bt=NK, owi=NK, o15i=8, CI=384)
+_sb(U16, u0=NK, u1=NK, wO=12, off=16, o15=8)
+_sb(F32, TB1=TBW, TB2=TBW, TB3=TBW, Z1c=NK, ZS0=512, ZS1=512, Mx=256, Ml=16, acc=12 * 193, rsd=386, off32=12, SRC=NK, SR2=NK, CF=384,
+    CM1=384, RC1=384, CM2=384, RC2=384, I32=128, nI32=128, nMV=96, segm=128, rst=128, pw=128, d0=128, d1=128, two=16, zer=16,
+    VR=[NCC, 2, 16], CC=32 * NCC, dum=12, dumr=12, yi=NK, TH=12)
+for _b in ("A0", "A1", "B0", "B1", "D0", "D1"):
     SCRATCH[_b] = ("psum", [128, 512], F32)
-NDS = 40
-SEMAPHORES = ["sV", "sS", "sP", "sG"] + ["d%d" % i for i in range(NDS)] + ["r%d" % i for i in range(6)] + ["l%d" % i for i in range(6)]
+SCRATCH["FF"] = ("psum", [128, 1024], F32)
+for _k in range(1, NST + 1):
+    _sb(F32, **{"RD%d" % _k: NK})
+    _sb(U16, **{"RO%d" % _k: 16})
+NDS, NRS = 60, 14
+SEMAPHORES = ["sV", "sS", "sP", "sG"] + ["d%d" % i for i in range(NDS)] + ["r%d" % i for i in range(NRS)] + ["l%d" % i for i in range(NRS)]
 HBM = {"turn": [8, NW], "twist": [128, NW], "img": [128, NK], "ent": [8, 2 * NW], "elen": [8, NW], "own": [8, 2 * NK],
        "olen": [8, NK], "yimg": [128, NK], "yf": [128, 3072], "yent": [8, 2 * NW], "yelen": [8, NW]}
 s_ = np.s_
-PAR = {"gv": (5,), "iv": (), "zp": ((0, 96),), "tb": 1600, "gc": 11, "cons": (2, 4, 6), "fs": (), "nb": 3}
-ORDER = r"021[010=000K0A1\0[0Z0I1a0O0W0D0E0B0Y0F0X0G0@0R1H0J031F0H1]0S1Q0U0P1>1L1O1S0>1;1T2L1G1P0\1N0Q041=1R0V0<2N1`0T0N0M250C1A202O1c06182P1_1M1V051:2>2T2Q0L261?2M1^1U2X2S2B0c2Y0;070i0:091W16080k1C10272:0l0e141<2?171I211B2U1X1J2;0n1E151b2Z0g281K2[0j1@2V2R0a2C2<0f29222f2\0_2W2g1D0o2=110]2@122]1h2^1Y0d0^2c2h0h2A2D2i0`1k1i2I131Z2_0?0m2j2E2`1j2a0b2b232J1o192H2F352G1d2d2k2e2K2l362m2n1e322o3334303f3O3N373h3g3i3M4D38391f3:3j3?243n1m3l3o3P1n3k3m3B3;401l3144414245463Q3@3<43474:484;4<3R493=3S3T1g4=3X3E3A4@3F4>3U4A3C4?3>3Y3[4B3V4C3D4H3^4G3G3Z4E4F3H3W4I3I3J3L3`4J3_3K3\4P4N4Q3a4R3]4K4S4L4T3e4O4U4M4]4V4W4[3b4X4^4Y3c4k4_3d4`4a4\4b4l4h4c4i4d4j5^4e5`4m5_4f5a5D5b4n6<505E5d5f5h54514g5e5g584o5i554Z6?5F59566=52575<5:535l5G5>5c5;5m5=5n5H5j6>625N5k5?5o605C615R5I6364665O675J656:6P686;5V6R5P5@6S5K5A695B6Q5X6@5W5Q6T5L6A6U5S6B6F6G5Y5T5M6H6J6I6V5Z5[5]6W6X6[6C6Y6^6Z6`6m6D6a5\6b6\6c6K5U6n6j6d6E6]6k6l6e7Z6f6g7\6o6h7[7D7]8870757C7^7b7`7d72767c7a7h7e7f7E6i737i6_7g7j777l787F7k717m89807G797_7I748B7;7:8:7n7L827<7J817o867H7O84837B87857M7K8<6L8=7N7R6M8>6O6N7=8C8F7P7S8G8;7T7>8H7Q7U7?7@8?8I7V8@7Y7A8J7W8K8S7X8T8D8L8E8Q8P8M8U8N8O8V8R8a8W8A8X8^8`8_8Y9T8Z8b8[9V:28\9U9W9:8c9<9Z8d9\9[9^8f9]9`9_9X9a9b9d9c8n9f8g9;8j9e9=8h8e8k9>9@9?9g9h8l9H9j8o9i9k9D9Y8]929n8m939L90949l8i9o:0999m:19E:>:@:3:A:5:6959F:491:79A96979N:89M9G:?9I9B:<98:9:=9O9J:::;:B:C9S9K:D:L:M:N9P:E:F:O:G:H:P9Q:[:J9R:Q:K:R:\:X:Y:S;H:T:Z9C:U;f:V;J;1;I;K;L;3;P:];Q;2;g;N:^;R;V:c;O;4;S:_;W:`:I;X;T:d;U:W;Y:f;Z:e;\:a;[;^;5:b:i;7;6:g;];_:k;`;=;8:j:h;b:l;a;:;9;0;c;d;@;i;h;M<9;e<:;><;:m;;;?:n;j;B;k:o;A;<<<;l;C<=<0<1;G<D<><F<3<4;D<2<G;E<?<H<C<@<I;F<A<J<B<Q<E<K<T;m;n;o<R<L=K<5<U<M<N=M=i<S=L=N<O=S=Q=1=T<V=R=j=U<W=Y=V=W<Y=Z=[=0=O=_<^<Z=X<o<c=]<_=P=\=o<P<[=k=2<6<8=^<\=`<`=a=e=3<]<d<7=5=b=f=:=c=g=d=6=4=h<X<a<e<h=l=7=?=m<i=;=n<f>0=8=@=<==<j=A=><b=9<g=D<k<l=B=E=F>1=C<m>2<n=G>4>5>3=H=I=J"
+PAR = {"pieces": ((0, 48, "S"), (48, 96, "V")), "raw": {4: ((0, 48, "S"), (48, 96, "T")), 6: ((0, 48, "S"), (48, 96, "U"))}, "whole": True, "q": ((0, 48, "V"), (48, 96, "V")), "ev": "SSS", "zp": ((0, 96),),
+       "mod1": (True, True), "init": ((0, 48, "S"), (48, 96, "V")), "ahead": (1, 1), "gc": 2, "tb": 1200, "last": "SV",
+       "eng": {"Ml": "V", "E": "S", "bt": "S", "b16": "S", "FL": "S", "Rr": "S", "Lm": "SS", "SRC": "S", "D": "SSSVVV", "b0": "S", "dump": "S", "mf": "S", "E0": "S"}, "pairs": (0, 3, 1, 4, 2, 5),
+       "beat": None, "gwake": 900, "swaps": 15000, "jump": 30, "heat": 300, "pull": 3, "rounds": 20, "noise": 1000, "ga": 1.5, "lead": {},
+       "first": {"Y": "b32 tw CI*3 owi*3 TB1*3 Wn*6 |", "S": "tni tw | npw TN*4 Wh*2 YT",
+                 "V": "onec zerc DW d0*2 d1*2 pw owi two zer VR*3 CC tnh TN | BP TB1",
+                 "G": "o15i ge JC dumr BO Ib DW S0 BO TN DW TN*3 TB1 |"}}
 
 
 def _shape(name):
@@ -65,7 +73,8 @@ def ind(win, offs):
 
 def build():
     ops = []
-    tag = ["i", 0]
+    tag, seen = [3, 0], {}
+    ENG = PAR["eng"]
 
     def add(eng, kind, args, reads, writes):
         rd, wr = [], []
@@ -78,7 +87,9 @@ def build():
             wr.append(_box(x))
             if len(x) == 3:
                 rd.append(_box(x[2]))
-        ops.append(dict(eng=eng, kind=kind, args=args, rd=rd, wr=wr, tag=tag[0], st=tag[1]))
+        name = "%s%s%s" % (eng, wr[0][0].rstrip("0123456"), tag[0])
+        seen[(name, tag[1])] = seen.get((name, tag[1]), -1) + 1
+        ops.append(dict(eng=eng, kind=kind, args=args, rd=rd, wr=wr, st=tag[1], name=name + "." + str(seen[(name, tag[1])])))
 
     def copy(out, in_):
         add("V", "copy", (out, in_), [in_], [out])
@@ -95,23 +106,37 @@ def build():
     def scan(out, x, y, init, o0, o1):
         add("V", "scan", (out, x, y, init, o0, o1), [x, y], [out])
 
+    def turn32(out, in_):
+        add("V", "vtr", (out, in_), [in_], [out])
+
     def act(out, in_, func=AF.Identity, bias=0.0, scale=1.0, accum=None):
         add("S", "act", (out, in_, func, bias, scale, accum), [in_, bias, scale], [out] + ([accum] if accum else []))
 
-    def scaled(out, in_, col):
-        act(out, in_, AF.Identity, 0.0, col)
-
-    def mm(lst):
-        add("P", "mm", lst, [x[1] for x in lst] + [x[2] for x in lst] + [x[0] for x in lst if not x[3]], [x[0] for x in lst])
-
-    def grp(items):
-        return [(o, l, r, k == 0, k == len(items) - 1) for k, (o, l, r) in enumerate(items)]
-
-    def iota(out, pat, base, cm):
+    def iota(out, pat, base, cm=0):
         add("G", "iota", (out, pat, base, cm), [], [out])
 
     def asel(out, in_, pat, cmp, fill, base, cm):
         add("G", "asel", (out, in_, pat, cmp, fill, base, cm), [in_], [out])
+
+    def lin(e, out, in_, bias=0.0, scale=1.0):
+        if e == "G":
+            asel(out, in_, [[0, _box(out)[4]]], A.is_ge, 0.0, 0, 0)
+        elif e == "S":
+            act(out, in_, AF.Identity, bias, scale)
+        elif scale == 1.0 and bias == 0.0:
+            copy(out, in_)
+        elif scale == 1.0:
+            ts(out, in_, bias, None, A.add)
+        else:
+            ts(out, in_, scale, bias, A.mult, A.add)
+
+    def mm(*parts, each=False):
+        parts = [x for x in parts if x]
+        for n, items in enumerate(parts):
+            lst = [(o, l, r, each or k == 0 == n, each or (k == len(items) - 1 and n == len(parts) - 1)) for k, (o, l, r) in enumerate(items)]
+            add("P", "mm", lst, [x[1] for x in lst] + [x[2] for x in lst], [x[0] for x in lst])
+            k = _box(lst[0][0])[2] // 512
+            ops[-1]["wr"].append(("turn of " + lst[0][0][0], frozenset([0]), k, k, 0))
 
     def dma(out, in_, q="Y"):
         add(q, "dma", (out, in_), [in_], [out])
@@ -123,279 +148,354 @@ def build():
         return ap("CC", s_[:, 32 * k:32 * k + 1])
 
     TROW = (0, 1, 11)
+    QB = 49152.0
 
-    dma(ap("b32"), ap("img"))
     dma(ap("tw", s_[:, 0:1024]), ap("twist", s_[:, 0:1024]))
     dma(ap("tw", s_[:, 1024:2048]), ap("twist", s_[:, 1024:2048]), "S")
+    dma(ap("b32"), ap("img"))
     dma(ap("tni", s_[0:32, :]), ap("turn"), "S")
     mset(ap("owi"), 0)
-    mset(ap("TB1", s_[:, PAR["tb"]:]), 0)
-    iota(ap("TB1", s_[:, 0:PAR["tb"]]), [[0, PAR["tb"]]], 0, 0)
     for k, (src, osrc) in enumerate(((ap("ent", s_[:, 0:NW]), ap("own", s_[:, 0:NK])), (ap("ent", s_[:, NW:]), ap("own", s_[:, NK:])),
                                      (ap("elen"), ap("olen")))):
-        dma(ap("TB1", s_[TROW[k]::16, 0:NW]), src)
+        dma(ap("CI", s_[:, 128 * k:128 * k + 128]), src)
         dma(ap("owi", s_[TROW[k]::16, :]), osrc)
+    mset(ap("TB1", s_[:, PAR["tb"]:]), 0.0)
+    iota(ap("TB1", s_[:, 0:PAR["tb"]]), [[0, PAR["tb"]]], 0)
+    lin("S", ap("CF", s_[:, 0:256]), ap("CI", s_[:, 0:256]))
+    lin("S", ap("CF", s_[:, 256:]), ap("CI", s_[:, 256:]), -2048.0)
+    for k in range(3):
+        dma(ap("TB1", s_[TROW[k]::16, 0:NW]), ap("CF", s_[:, 128 * k:128 * k + 128]))
 
     mset(ap("onec"), 1.0)
-    mset(ap("oneb", s_[0:32, :]), 1.0)
-    mset(ap("big", s_[0:32, :]), 49152.0)
-    asel(ap("Ic"), ap("onec"), [[-1, 128]], A.is_equal, 0.0, 0, 1)
+    mset(ap("zerc"), 0.0)
+    asel(ap("Ib"), ap("onec"), [[-1, 128]], A.is_equal, 0.0, 0, 1)
     asel(ap("BO"), ap("onec"), [[-16, 8], [0, 16]], A.is_ge, 0.0, 0, 1)
     asel(ap("BO"), ap("BO"), [[16, 8], [0, 16]], A.is_ge, 0.0, 15, -1)
-    asel(ap("Sub"), ap("onec"), [[-1, 128]], A.is_equal, 0.0, -1, 1)
-    mset(ap("segm"), 1.0)
-    mset(ap("segm", s_[:, 0::16]), 0.0)
-    act(ap("d0"), ap("segm"), AF.Identity, 0.0, 0.5)
-    ts(ap("d1"), ap("segm"), -1.0, 1.0, A.mult, A.add)
+    for nm, v, v0 in (("d0", 0.5, 0.0), ("d1", 0.0, 1.0)):
+        mset(ap(nm), v)
+        mset(ap(nm, s_[:, 0::16]), v0)
+    lin("S", ap("rst"), ap("d1"), 0.0, -2.0 ** 22)
     scan(ap("pw"), ap("d0"), ap("d1"), 0.0, A.mult, A.add)
     mset(ap("two"), 2.0)
     mset(ap("zer"), 0.0)
-    mset(ap("VR", s_[:, 0:320]), 0.0)
-    mset(ap("VR", s_[:, 320:]), 0.0)
+    mset(ap("VR"), 0.0)
 
-    def vr(k, t0, t1, v, go=None):
-        if go is None and t1 - t0 == 1:
-            parts = [ap("VR", s_[:, 32 * k + t0:32 * k + 32:16])]
+    def vr(k, t0, t1, v, o=slice(None)):
+        x = ap("VR", s_[:, k, o, t0:t1])
+        if k < PAR["gc"]:
+            mset(x, v)
+        elif v == int(v):
+            iota(x, [[0, _box(x)[4]]], int(v))
         else:
-            parts = [ap("VR", s_[:, 32 * k + 16 * o + t0:32 * k + 16 * o + t1]) for o in ((0, 1) if go is None else (go,))]
-        for x in parts:
-            if k >= PAR["gc"]:
-                iota(x, [[0, _box(x)[4]]], int(v), 0)
-            else:
-                mset(x, v)
+            asel(x, x, [[0, _box(x)[4]]], A.not_equal, v, 0, 0)
     for o in (0, 1):
-        scan(ap("VR", s_[:, 16 * o:16 * o + 11]), ap("two", s_[:, 0:11]), ap("zer", s_[:, 0:11]), 2.0 ** -9, A.mult, A.add)
-    vr(1, 0, 1, 1.0); vr(2, 0, 1, -1.0); vr(2, 1, 2, 1.0); vr(3, 11, 12, 1.0); vr(4, 11, 12, -2048.0); vr(5, 11, 12, 2048.0)
-    vr(6, 0, 11, 1.0); vr(7, 1, 12, -2.0); vr(8, 0, 2, 1.0); vr(9, 12, 13, 1.0 / 256); vr(9, 14, 15, 1.0 / 256)
-    ts(ap("VR", s_[:, 320:352]), ap("pw", s_[:, 0:32]), 0.5, 1023.5, A.mult, A.add)
-    vr(10, 0, 1, 0.0); vr(18, 1, 32, 1024.0, 0); vr(18, 0, 1, 0.0, 1)
-    vr(11, 0, 11, 128.0); vr(11, 11, 13, 1.0)
-    vr(12, 0, 1, 128.0 * 2048 - 64); vr(12, 1, 11, 128.0 * 1024 - 64); vr(12, 13, 15, 1.0); vr(12, 15, 16, 64.0)
+        scan(ap("VR", s_[:, 0, o, 0:11]), ap("two", s_[:, 0:11]), ap("zer", s_[:, 0:11]), 2.0 ** -9, A.mult, A.add)
+    turn32(ap("CC", s_[:, 0:32]), ap("VR", s_[:, 0]))
+    ts(ap("VR", s_[:, 1]), ap("pw", s_[:, 0:32]), 0.5, 1535.5, A.mult, A.add)
+    vr(1, 0, 1, 0.0); vr(1, 1, 2, 1023.75)
+    bits = ((0, 2, 128 * 2048 - 64), (2, 11, 128 * 1536 - 64))
+    vr(2, 0, 11, -0.5); vr(2, 11, 13, 1)
+    for (t0, t1, v) in bits + ((11, 12, 2), (13, 15, 1)):
+        vr(3, t0, t1, v)
     for o in (0, 1):
-        vr(13 + 2 * o, 0, 11, -64.0, o); vr(13 + 2 * o, 13, 15, -1.0, o)
-        vr(14 + 2 * o, 0, 1, 32 - 64.0 * 2048, o); vr(14 + 2 * o, 1, 11, 32 - 64.0 * 1024, o)
-        vr(14 + 2 * o, 11, 13, 1.0, o); vr(14 + 2 * o, 15, 16, 352.0, o)
-    iota(ap("VR", s_[:, 544:576]), [[0, 2], [1, 16]], 0, 0)
-    add("V", "vtr", (ap("CC", s_[:, 0:320]), ap("VR", s_[:, 0:320])), [ap("VR", s_[:, 0:320])], [ap("CC", s_[:, 0:320])])
-    add("V", "vtr", (ap("CC", s_[:, 320:]), ap("VR", s_[:, 320:])), [ap("VR", s_[:, 320:])], [ap("CC", s_[:, 320:])])
+        vr(4 + 2 * o, 0, 11, -0.5, o); vr(4 + 2 * o, 13, 15, 1, o); vr(4 + 2 * o, 15, 16, -1, o)
+        for (t0, t1, v) in bits + ((11, 13, -1), (13, 14, 2)):
+            vr(5 + 2 * o, t0, t1, v, o)
+    iota(ap("VR", s_[:, 8]), [[0, 2], [1, 16]], 0)
+    vr(9, 11, 12, -45056); vr(9, 12, 13, -0.5); vr(9, 13, 14, 1); vr(9, 15, 16, 1)
+    turn32(ap("CC", s_[:, 32:]), ap("VR", s_[:, 1:]))
     BM = ap("BO", s_[:, 0::16])
-    scaled(ap("Ib"), ap("Ic"), 1.0); scaled(ap("nIb"), ap("Ic"), -1.0); scaled(ap("nIc"), ap("Ic"), -1.0)
-    scaled(ap("I32"), ap("Ic"), 1.0); scaled(ap("nI32"), ap("Ic"), -1.0)
-    for nm, col in (("BigZ", cc(0)), ("Big1", 1.0), ("BigL", cc(3))):
+    lin("S", ap("I32"), ap("Ib")); lin("S", ap("nI32"), ap("Ib"), 0.0, -1.0)
+    asel(ap("nIb"), ap("zerc"), [[-1, 128]], A.not_equal, -1.0, 0, 1)
+    asel(ap("Fold"), ap("zerc"), [[-1, 128]], A.not_equal, 8192.0, 0, 1)
+    for nm, col in (("BigZ", cc(0)), ("Big1", 1.0)):
         mset(ap(nm), 0.0)
-        scaled(ap(nm, s_[:, 15:143:16]), BM, col)
-    scaled(ap("Wh", s_[:, 0:8]), BM, cc(0)); scaled(ap("Wh", s_[:, 8:16]), BM, 1.0)
-    scaled(ap("Wq"), BM, -1.0); scaled(ap("W0"), BM, 1.0)
-    scaled(ap("S0"), ap("BO"), cc(1)); scaled(ap("S10"), ap("BO"), cc(2)); scaled(ap("nS0"), ap("S0"), -1.0)
+        lin("S", ap(nm, s_[:, 15:143:16]), BM, 0.0, col)
+    lin("S", ap("Wh", s_[:, 0:8]), BM, 0.0, cc(0)); lin("S", ap("Wh", s_[:, 8:16]), BM); lin("S", ap("Wq"), BM, 0.0, -1.0)
     tt(ap("BP"), ap("BO"), ap("pw"), A.mult)
-    scaled(ap("YT"), ap("BP"), cc(0))
+    lin("S", ap("YT"), ap("BP"), 0.0, cc(0))
+    lin("S", ap("npw", s_[0:32, :]), ap("pw", s_[0:32, :]), 0.0, -1.0)
+    mset(ap("tnh", s_[32:64, :]), 1.0)
+    mset(ap("TN", s_[32:64, :]), -0.5)
     for k in range(4):
-        scaled(ap("npw", s_[0:32, 128 * k:128 * k + 128]), ap("pw", s_[0:32, :]), -1.0)
-    asel(ap("TN", s_[0:32, :]), ap("npw", s_[0:32, :]), [[-1, 4], [-4, 8], [0, 16]], A.is_equal, 0.0, 0, 1)
-    scaled(ap("CO", s_[0:32, :]), ap("pw", s_[0:32, :]), 2.0 ** -9)
-    asel(ap("CO", s_[0:32, :]), ap("CO", s_[0:32, :]), [[0, 128]], A.is_equal, -0.5, -1, 1)
-    scaled(ap("Dt"), ap("Sub"), cc(7)); scaled(ap("Dm"), ap("Ic"), cc(6))
-    tt(ap("Dm"), ap("Dm"), ap("Dt"), A.add)
-    scaled(ap("DW"), ap("Dm"), -256.0)
-    scaled(ap("Sel01"), ap("Ic"), cc(8)); scaled(ap("Sel11"), ap("Ic"), cc(3))
-    iota(ap("tier"), [[0, 8], [-1, 16]], 16, 0)
-    scaled(ap("tie"), ap("tier"), 1.0 / 16)
-    iota(ap("o15i"), [[16, 8]], 15, 0)
+        asel(ap("TN", s_[0:32, 128 * k:128 * k + 128]), ap("npw", s_[0:32, :]), [[-4, 8], [0, 16]], A.is_equal, 0.0, -k, 1)
+        lin("S", ap("TN", s_[32:33, 128 * k:128 * k + 128]), ap("pw", s_[32:33, :]), 0.0, 2.0 ** -9)
+    mset(ap("DW"), 0.0)
+    for k, v in ((0, -256.0), (1, 512.0)):
+        asel(ap("DW", s_[:, :, 0:11]), ap("DW", s_[:, :, 0:11]), [[-16, 8], [-1, 11]], A.not_equal, v, -k, 1)
+
+    def link_rows(out, in_, t, t2, v):
+        asel(ap(out), ap(in_), [[-16, 8], [0 if t2 is None else 128, 16]], A.not_equal, v, -t - 128 * (t2 or 0), 1)
+    link_rows("S0", "zerc", 0, None, 1.0); link_rows("nS0", "zerc", 0, None, -1.0); link_rows("S10", "nS0", 1, None, 1.0)
+    link_rows("nS1", "zerc", 1, None, -1.0)
+    link_rows("SelL", "zerc", 11, 15, 1.0); link_rows("Sel11", "zerc", 11, 11, 1.0); link_rows("SelM", "Sel11", 11, 13, 1.0)
+    link_rows("Sel01", "Ib", 11, 11, 0.0); link_rows("SelJ", "zerc", 0, 12, 1.0 / 256); link_rows("SelJ", "SelJ", 0, 14, 1.0 / 256)
+    v0 = min(l0 for (l0, l1, t) in PAR["pieces"] if t == "V")
+    asel(ap("nMV", s_[0:96, :]), ap("nI32", s_[0:96, 0:96]), [[1, 96]], A.is_ge, 0.0, -v0, 0)
+    iota(ap("o15i"), [[1, 8]], 0)
     copy(ap("o15"), ap("o15i"))
-    mset(ap("Kk", s_[96:128, :]), 0.0); mset(ap("Mx", s_[96:128, :]), 0.0)
-    iota(ap("Jf"), [[1, NK]], 0, 0)
-    scaled(ap("JC"), ap("Jf"), cc(9))
-    iota(ap("dumr"), [[16, 12]], NW, 0)
-    ts(ap("dum"), ap("dumr"), cc(17), None, A.add)
-    copy(ap("o4i"), ap("dum", s_[:, 0:4]))
-    ts(ap("o4i"), ap("o4i"), 2, 511, A.logical_shift_right, A.bitwise_and)
-    copy(ap("o4"), ap("o4i"))
-    iota(ap("TH"), [[0, 48]], 0, 0)
-    asel(ap("TH"), ap("TH"), [[0, 12], [-32, 4]], A.is_ge, 1e9, 0, 1)
-    asel(ap("TH"), ap("TH"), [[0, 12], [32, 4]], A.is_ge, 1e9, 31, -1)
-    mset(ap("Fold"), 0.0)
-    for x in range(4):
-        scaled(ap("Fold", s_[32 * x:32 * x + 32, 96:128]), ap("Ic", s_[32 * x:32 * x + 32, 32 * x:32 * x + 32]), 8192.0)
-    mset(ap("EX"), 0.0)
-    for t in (11, 13):
-        asel(ap("EX", s_[:, t::16]), ap("onec"), [[-1, 16], [-16, 8]], A.is_equal, 0.0, 0, 1)
-    iota(ap("TB2"), [[0, TBW]], 0, 0)
-    iota(ap("TB3"), [[0, TBW]], 0, 0)
+    for c in range(2):
+        lin("S", ap("Mx", s_[96:128, 128 * c:128 * c + 128]), ap("pw", s_[96:128, :]), 0.0, -1.0)
+    iota(ap("ge", s_[:, 15::144]), [[0, 2]], 1)
+    lin("S", ap("nI1", s_[0:96, :]), ap("Ib", s_[0:96, 0:96]), 0.0, -1.0)
+    mset(ap("nI1", s_[96:97, :]), 1.0)
+    iota(ap("JC"), [[1, NK]], 0)
+    mset(ap("neg2"), -2.0)
+    iota(ap("dumr"), [[16, 12]], NW)
+    ts(ap("dum"), ap("dumr"), cc(8), None, A.add)
+    mset(ap("off"), 0)
+    lin("G", ap("Rr", s_[:, 192:193]), cc(9))
+    if "V" in ENG["D"]:
+        for e, n0, n1 in [(e, n, n + len(e)) for n, e in ((0, ENG["D"].rstrip("V")), (len(ENG["D"].rstrip("V")), ENG["D"].lstrip("S"))) if e]:
+            iota(ap("TH", s_[:, 2 * n0:2 * n1]), [[0, 2 * (n1 - n0)]], 0 if e[0] == "S" else 45056)
+        iota(ap("rsd"), [[0, 386]], 0)
+        iota(ap("rsd", s_[:, 0::193]), [[0, 2]], -2 ** 22)
+    for nm in ("TB2", "TB3"):
+        for k in range(0, TBW, 560):
+            iota(ap(nm, s_[:, k:k + 560]), [[0, 560]], 0)
+    iota(ap("mid"), [[0, NK]], 2048)
+    iota(ap("high", s_[0:32, :]), [[0, 128]], int(QB))
+    iota(ap("ones", s_[0:32, :]), [[0, 512]], 1)
 
     copy(ap("tnh", s_[0:32, :]), ap("tni", s_[0:32, :]))
     MAG = 1.5 * 2 ** 23
     for k in range(4):
         cs = s_[:, 512 * k:512 * k + 512]
-        yb = ap("F%d" % k)
-        mm(grp([(yb, ap("YT"), ap("tw", cs)), (yb, ap("TN", s_[0:32, 128 * k:128 * k + 128]), ap("tnh", s_[0:32, :])),
-                (yb, ap("CO", s_[0:2, :]), ap("oneb", s_[0:2, :]))]))
+        yb = ap("FF", s_[:, 512 * (k % 2):512 * (k % 2) + 512])
+        mm([(yb, ap("YT"), ap("tw", cs))], [(yb, ap("TN", s_[0:34, 128 * k:128 * k + 128]), ap("tnh", s_[0:34, :]))])
         ts(ap("FLW", cs), yb, MAG, MAG, A.add, A.subtract)
-        wb = ap("F%d" % (4 + k % 2))
-        mm(grp([(wb, ap("Ib"), ap("tw", cs)), (wb, ap("DW"), ap("FLW", cs))]))
+        wb = ap(("D0", "D1")[k % 2])
+        mm([(wb, ap("Ib"), ap("tw", cs))], [(wb, ap("DW"), ap("FLW", cs))])
         act(ap("Wn", cs), wb)
-    for k in (1, 2, 3):
-        dma(ap("Wn", s_[:, k * NW:(k + 1) * NW]), ap("Wn", s_[:, 0:NW]))
+        if k % 2:
+            for n in (1, 2, 3):
+                dma(ap("Wn", s_[:, n * NW + 512 * k - 512:n * NW + 512 * k + 512]), ap("Wn", s_[:, 512 * k - 512:512 * k + 512]))
 
-    def ln(name, c):
-        return ap(name, s_[:, 96 * c:96 * c + 96])
+    def ln(name, c, l0=0, l1=96):
+        return ap(name, s_[:, 96 * c + l0:96 * c + l1])
 
-    def lm(name, c, p=96):
-        return ap(name, s_[0:p, 128 * c:128 * c + 128])
+    def big(name, c, l0, l1):
+        return ap(name, s_[:, 1536 * c + 16 * l0:1536 * c + 16 * l1])
+
+    def pa(c, a, b, p=128, st=None):
+        return ap("A%d" % c, s_[0:p, a:b:st])
 
     def pb(c, a, b, p=128, st=None):
-        return ap("P%d" % c, s_[0:p, a:b:st])
+        return ap("B%d" % c, s_[0:p, a:b:st])
 
-    def qb(c, a, b, p=128, st=None):
-        return ap("F%d" % (PAR["nb"] + c), s_[0:p, a:b:st])
+    def im(name, c, i, l0=0, l1=96):
+        return ap(name, s_[:, 1536 * c + 16 * l0 + i:1536 * c + 16 * l1:16])
 
-    def im(name, c, i):
-        return ap(name, s_[:, 1536 * c + i:1536 * c + 1536:16])
+    def zs(n, c, a, b):
+        return ap("ZS%d" % (n % 2), s_[0:96, 256 * c + a:256 * c + b])
 
-    def diag(big, rhs, out):
-        return [(out, ap(big, s_[:, 15 - k:143 - k]), rhs(k)) for k in range(16)]
+    def diag(big_, rhs, out):
+        return [(out, ap(big_, s_[:, 15 - k:143 - k]), rhs(k)) for k in range(16)]
 
-    ts(ap("E0"), ap("owi"), cc(4), None, A.add)
-    mm(grp(diag("BigL", lambda k: ap("E0", s_[:, k::16]), pb(1, 448, 460))))
-    copy(ap("m0"), pb(1, 448, 460))
+    def turned(n, c, nf):
+        mm([(pb(c, 96 + i, 96 + 16 * nf, 96, 16), im("X", c, i), ap("Wh", s_[:, 0:nf])) for i in range(16)], each=True)
+        act(zs(n, c, 0, 16 * nf), pb(c, 96, 96 + 16 * nf, 96))
+
+    nb = [0]
+
+    def summed(c, l0, l1, terms, high=False, banks=None):
+        nb[0] += 1
+        name, k0 = banks or ("FF", 512 * (nb[0] % 2) if l1 - l0 <= 32 else 0)
+        for l in range(l0, l1, 32):
+            m = min(l + 32, l1)
+            f = ap(name, s_[:, k0 + 16 * (l - l0):k0 + 16 * (m - l0)])
+            lst = [(f, ap("high", s_[0:1, :]), ap("ones", s_[0:1, 0:16 * (m - l)]))] if high else []
+            lst += [(f, ap(w), big(v, c, l, m)) for (w, v) in terms]
+            mm(lst[:-1], lst[-1:])
+        return ap(name, s_[:, k0:k0 + 16 * (l1 - l0)])
+
+    def ahead(tb, cm, rc, nx):
+        for k in range(3 if tb else 0):
+            dma(ap(cm, s_[:, 128 * k:128 * k + 128]), ap(tb, s_[TROW[k]::16, 0:NW]))
+        remote(ap(rc), ap(cm))
+        if nx == "TB3":
+            lin("S", ap(rc, s_[:, 256:]), ap(rc, s_[:, 256:]), 2048.0)
+        for k in range(3):
+            dma(ap(nx, s_[TROW[k]::16, 0:NW]), ap(rc, s_[:, 128 * k:128 * k + 128]))
+
+    lin(ENG["E0"], ap("E0"), ap("owi"))
+    lin("S", ap("mf"), ap("owi"), -2048.0)
     copy(ap("u1"), ap("b32"))
-    copy(ap("b16"), ap("b32"))
+    lin(ENG["b0"], ap("b16"), ap("b32"))
     for c in range(2):
-        for p in range(2):
-            (copy if 2 * c + p in PAR["iv"] else act)(ap("fb", s_[:, 1536 * c + 768 * p:1536 * c + 768 * p + 768]),
-                                                      ind(ap("tw"), ap("u1", s_[:, 96 * c + 48 * p:96 * c + 48 * p + 48])))
-        mm([(pb(c, i, 128, 96, 16), im("fb", c, i), ap("W0"), True, True) for i in range(16)])
-        tt(lm("Kk", c), pb(c, 0, 128, 96), ap("tie", s_[0:96, :]), A.add)
-        act(lm("Aa", c), lm("Kk", c), AF.Identity, 16 * 49152.0)
-    held = []
+        for (l0, l1, e) in PAR["init"]:
+            lin(e, big("X", c, l0, l1), ind(ap("tw"), ln("u1", c, l0, l1)))
+        turned(0, c, 16)
+    if PAR["ahead"][0] == 0:
+        ahead(None, "CF", "RC1", "TB2")
 
     OFF = 4096 - 127.5 / 256
+
+    def choose(st, c):
+        TB, En = "TB1" if st <= NEV else "TB2", "E%d" % (st % 2)
+        mx = ap("Mx", s_[:, 128 * c:128 * c + 128])
+        K = zs(0, c, 128, 256) if st == 1 else pb(c, 352, 480, 96)
+        scan(ap("Mx", s_[0:96, 128 * c:128 * c + 128]), ap("rst", s_[0:96, :]), K, 0.0, A.add, A.max)
+        g0 = 144 * c + 16
+        ml = ap("Ml", s_[:, 8 * c:8 * c + 8])
+        lin(ENG["Ml"], ml, ap("Mx", s_[:, 128 * c + 15:128 * c + 128:16]))
+        tt(ap("ge", s_[:, g0:g0 + 128]), ind(ml, ap("o15")), mx, A.is_equal)
+        mm([(pa(c, 128, 224), ap("ge", s_[0:96, g0:g0 + 128]), ap("Ib", s_[0:96, 0:96])),
+            (pa(c, 128, 224), ap("ge", s_[0:97, g0 - 1:g0 + 127]), ap("nI1", s_[0:97, :]))])
+        tt(ln("Am", c), pa(c, 128, 224), ln("b32", c), A.mult)
+        mm(diag("Big1", lambda k: ap("Am", s_[:, 96 * c + k:96 * c + 96:16]), pa(c, 224, 230)))
+        wo = ap("wO", s_[:, 6 * c:6 * c + 6])
+        copy(wo, pa(c, 224, 230))
+        lin(ENG["E"], ln(En, c), ind(ap(TB, s_[:, 0:NW]), wo))
+        act(ap("wf", s_[:, 6 * c:6 * c + 6]), pa(c, 224, 230))
+        mm([(pa(c, 256, 352), ap("Ib"), ln("b16", c))], [(pa(c, 256, 352), ap("S0"), ln(En, c))])
+        if st == 1 and PAR["mod1"][0]:
+            copy(ln("bt", c), pa(c, 256, 352))
+            ts(ln("bt", c), ln("bt", c), NW - 1, None, A.bitwise_and)
+            copy(ln("u0", c), ln("bt", c))
+        else:
+            copy(ln("u0", c), pa(c, 256, 352))
+
+    def letters(st, c):
+        En = "E%d" % (st % 2)
+        raw = st in PAR["raw"]
+        pieces = PAR["raw"][st] if raw else PAR["pieces"]
+        kept = [l0 for (l0, l1, t) in pieces if t in "VWT"]
+        w0 = ap("Wn", s_[:, 0:NW if st == 1 and PAR["mod1"][0] else 2 * NW])
+        w1 = ap("Wn", s_[:, 0:NW if st == 1 and PAR["mod1"][1] else 4 * NW])
+        for (l0, l1, t) in pieces:
+            if t in "VWT":
+                tt(big("Y", c, l0, l1), ind(w0, ln("u0", c, l0, l1)), big("X", c, l0, l1), A.add)
+            else:
+                lin("V" if t in "QU" else "S", big("Y", c, l0, l1), ind(w0, ln("u0", c, l0, l1)))
+        for (l0, l1) in PAR["zp"]:
+            z = pb(c, l0, l1)
+            old = [] if not kept or l1 <= v0 else [(z, zs(st - 1, c, 0, 128), ap("nMV", s_[0:96, l0:l1]))]
+            mm(old + [(z, ap("S10"), ln(En, c, l0, l1))], diag("BigZ", lambda i: im("Y", c, i, l0, l1), z))
+            if st == 1 and PAR["mod1"][1]:
+                ts(ln("bt", c, l0, l1), z, OFF, None, A.add)
+                ts(ln("bt", c, l0, l1), ln("bt", c, l0, l1), NW - 1, None, A.bitwise_and)
+                copy(ln("u1", c, l0, l1), ln("bt", c, l0, l1))
+            else:
+                ts(ln("u1", c, l0, l1), z, OFF, None, A.add)
+        if not raw:
+            act(ln("Z1c", c), pb(c, 0, 96))
+        for p, (l0, l1, t) in enumerate(pieces):
+            x, y, q, fd = (big(nm, c, l0, l1) for nm in ("X", "Y", "qq", "FD"))
+            if t == "V":
+                tt(x, ind(w1, ln("u1", c, l0, l1)), y, A.add)
+                continue
+            lin("V" if t in "RUT" else "S", fd, ind(w1, ln("u1", c, l0, l1)))
+            terms = ([] if t in "WT" else [("Ib", "X")]) + ([("nIb", "qq")] if st == NEV + 1 else []) + [("Ib", "Y"), ("Ib", "FD")]
+            if st < NST:
+                for (l, m) in ((l0, l1),) if PAR["whole"] else [(l, min(l + 32, l1)) for l in range(l0, l1, 32)]:
+                    lin(PAR["ev"][p], big("X", c, l, m), summed(c, l, m, terms), QB if st == NEV + 1 else 0.0)
+                continue
+            for n, l in enumerate(range(l0, l1, 32)):
+                m = min(l + 32, l1)
+                f = summed(c, l, m, terms, True, (("B%d" % c, 0), None)[(n + p) % 2])
+                lin(PAR["last"][0], big("qq", c, l, m), f, -127.5)
+                tt(big("fo", c, l, m), f, big("qq", c, l, m), A.subtract)
+            dma(big("yf", c, l0, l1), big("fo", c, l0, l1))
+        z = pa(c, 352, 448)
+        if st < NST:
+            for (l0, l1, e) in PAR["q"]:
+                lin(e, big("qq", c, l0, l1), big("X", c, l0, l1), QB - 127.5)
+            turned(st, c, 16)
+        if raw:
+            mm([(z, ap("nS1"), ln(En, c))], diag("BigZ", lambda i: im("FD", c, i), z))
+        else:
+            mm([(z, zs(st - 1, c, 0, 128), ap("nI32", s_[0:96, 0:96])), (z, ap("nI32"), ln("Z1c", c)), (z, ap("nS0"), ln(En, c))],
+               [(z, zs(st, c, 0, 128), ap("I32", s_[0:96, 0:96]))])
+        lin(ENG["bt"], ln("bt", c), z, OFF)
+        ts(ln("b32", c), ln("bt", c), NW - 1, None, A.bitwise_and)
+        if st < NST:
+            mm([(pb(c, 352, 480, 96), ap("I32", s_[0:96, 0:96]), zs(st, c, 128, 256))],
+               [(pb(c, 352 + i, 480, 96, 16), im("qq", c, i), ap("Wq")) for i in range(16)])
+            lin(ENG["b16"], ln("b16", c), ln("b32", c))
+        else:
+            lin("S", ln("yi", c), ln("b32", c))
+            dma(ln("yimg", c), ln("yi", c))
+
+    def winners(st):
+        ep = (st - 1) // NEV
+        TB, NX, En, Ep = "TB%d" % (ep + 1), "TB%d" % (ep + 2), "E%d" % (st % 2), "E%d" % (1 - st % 2)
+        Xb = ap("D0", s_[:, 0:192])
+        mm([(ap("D1", s_[:, 0:192]), ap("BP"), ap("Am"))])
+        lin(ENG["FL"], ap("FL"), ap("D1", s_[:, 0:192]), cc(1))
+        mm([(Xb, ap("SelM"), ap("mf")), (Xb, ap("SelJ"), ap("JC"))] + ([(Xb, ap("SelM"), ap("neg2"))] if st == 1 else []),
+           [(Xb, ap("SelL"), ap(En))], [(Xb, ap("DW"), ap("FL"))])
+        lin(ENG["Rr"], ap("Rr", s_[:, 0:192]), Xb, cc(3), cc(2))
+        for o in (0, 1):
+            lin(ENG["Lm"][o], ap("Lm", s_[:, :, 16 * o:16 * o + 16]), Xb, cc(5 + 2 * o), cc(4 + 2 * o))
+        dump = ap(TB, s_[:, NW:])
+        sent = (st - 1) % NEV >= PAR["ahead"][ep]
+        Sb = ap("D1", s_[:, 200:392])
+        words = [(Sb, ap("Sel01"), ap(Ep)), (Sb, ap("Sel11"), ap("Rr", s_[:, 0:192]))]
+        if st < NST:
+            lin(ENG["dump"], dump, ap(En))
+            mm(words)
+            lin(ENG["SRC"], ap("SRC"), Sb)
+        if sent and ep == 1:
+            mm([(Sb, ap("Sel11"), ap("mid"))] + words)
+            lin(ENG["SRC"], ap("SR2"), Sb)
+        if sent:
+            remote(ap("RD%d" % st), ap(("SRC", "SR2")[ep]))
+        for u, n in enumerate(PAR["pairs"]):
+            bank = "D%d" % (u % 2)
+            for k in (2 * n, 2 * n + 1):
+                a, cb = k // 3, k % 3
+                mm([(ap(bank, s_[:, 193 * (k % 2):193 * (k % 2) + 193]), ap("Lm", s_[32 * a:32 * a + 32, 4 * cb:4 * cb + 4, :]),
+                     ap("Rr", s_[32 * a:32 * a + 32, 0:193]))])
+                ops[-1]["fence"] = k % 2 == 1 and cb == 0
+            if ENG["D"][n] == "V":
+                scan(ap("acc", s_[:, 386 * n:386 * n + 386]), ap("rsd"), ap(bank, s_[:, 0:386]), 0.0, A.add, A.max)
+            for k in (2 * n, 2 * n + 1) if ENG["D"][n] == "S" else ():
+                act(ap("junk", s_[:, 200 * (k % 2):200 * (k % 2) + 193]), ap(bank, s_[:, 193 * (k % 2):193 * (k % 2) + 193]), AF.Relu,
+                    -45056.0, 1.0, ap("acc", s_[:, 193 * k + 192:193 * k + 193]))
+        if "V" in ENG["D"]:
+            tt(ap("flag"), ap("acc", s_[:, 192::193]), ap("TH"), A.is_gt)
+        else:
+            act(ap("flag"), ap("acc", s_[:, 192::193]), AF.Sign)
+        Yb = ap("D0", s_[:, 400:412])
+        for a in range(4):
+            mm([(ap("D0", s_[32 * a:32 * a + 32, 400:412]), ap("Ib", s_[:, 32 * a:32 * a + 32]), ap("wf"))]
+               + [(ap("D0", s_[32 * a:32 * a + 32, 400 + x:412:4]), ap("Fold", s_[:, 32 * x:32 * x + 32]),
+                   ap("flag", s_[:, 3 * a:3 * a + 3])) for x in range(4)])
+        tt(ap("off32"), Yb, ap("dum"), A.min)
+        off = ap("off", s_[:, 0:12])
+        copy(off, ap("off32"))
+        if sent:
+            remote(ap("RO%d" % st), ap("off"))
+        if st < NST:
+            copy(ind(ap(TB), off), ap("SRC"))
+            lin(ENG["mf"], ap("mf"), dump)
+        if sent:
+            copy(ind(ap(NX), ap("RO%d" % st, s_[:, 0:12])), ap("RD%d" % st))
+        if (ep, st - NEV * ep) == (0, PAR["ahead"][0]):
+            ahead("TB1", "CM1", "RC1", "TB2")
+        if st - NEV == PAR["ahead"][1]:
+            ahead("TB2", "CM2", "RC2", "TB3")
+
     for st in range(1, NST + 1):
         tag[1] = st
-        hh = "hh%d" % len(held)
-        held.append(hh)
-        cons = st in PAR["cons"]
-        TB = "TB1" if st <= NEV else "TB2"
-        En, Ep = "E%d" % (st % 2), "E%d" % (1 - st % 2)
-        mo, mn = "m%d" % (1 - st % 2), "m%d" % (st % 2)
-        for c in range(2):
-            tag[0] = "a%d" % c
-            if st > 1:
-                tt(lm("Kk", c), pb(c, 0, 128, 96), lm("Aa", c), A.add)
-                if st - 1 in PAR["cons"] and st < NST:
-                    act(lm("Aa", c), lm("Kk", c), AF.Identity, 16 * 49152.0)
-            scan(lm("Mx", c), ap("segm", s_[0:96, :]), lm("Kk", c), 0.0, A.mult, A.max)
-            tt(lm("eq", c, 128), ind(lm("Mx", c, 128), ap("o15")), lm("Kk", c, 128), A.is_equal)
-            mm([(pb(c, 0, 96), lm("eq", c), ap("Ib", s_[0:96, 0:96]), True, True)])
-            tt(ln("Am", c), pb(c, 0, 96), ln("b16", c), A.mult)
-            mm(grp(diag("Big1", lambda k: ap("Am", s_[:, 96 * c + k:96 * c + 96:16]), pb(c, 224, 230))))
-            wo = ap("wO", s_[:, 6 * c:6 * c + 6])
-            copy(wo, pb(c, 224, 230))
-            ts(ln(En, c), ind(ap(TB), wo), cc(4), None, A.add)
-            mm(grp([(pb(c, 0, 96), ap("Ic"), ln("b16", c)), (pb(c, 0, 96), ap("S0"), ln(En, c))]))
-            if st > 1:
-                copy(ln("u0", c), pb(c, 0, 96))
-            else:
-                copy(ln("bt", c), pb(c, 0, 96))
-                ts(ln("bt", c), ln("bt", c), NW - 1, None, A.bitwise_and)
-                copy(ln("u0", c), ln("bt", c))
-            act(ap("wf", s_[:, 6 * c:6 * c + 6]), pb(c, 224, 230))
-            mm([(pb(c, 128, 224), ap("BP"), ln("Am", c), True, True)])
-            ts(ln("FL", c), pb(c, 128, 224), cc(10), cc(18), A.add, A.max)
-        for c in range(2):
-            tag[0] = "b%d" % c
-            for k in range(3 * c, 3 * c + 3):
-                (copy if k in PAR["gv"] else act)(ap("ga", s_[:, 512 * k:512 * k + 512]),
-                                                  ind(ap("Wn", s_[:, 0:2 * NW if st > 1 else NW]), ap("u0", s_[:, 32 * k:32 * k + 32])))
-            for (l0, l1) in PAR["zp"]:
-                z, cl = pb(c, l0, l1), s_[:, 96 * c + l0:96 * c + l1]
-                mm(grp(diag("BigZ", lambda i: ap("ga", s_[:, 1536 * c + 16 * l0 + i:1536 * c + 16 * l1:16]), z) + [(z, ap("S10"), ap(En, cl))]))
-                if st > 1:
-                    ts(ap("u1", cl), z, OFF, None, A.add)
-                else:
-                    ts(ap("bt", cl), z, OFF, None, A.add)
-                    ts(ap("bt", cl), ap("bt", cl), NW - 1, None, A.bitwise_and)
-                    copy(ap("u1", cl), ap("bt", cl))
-            act(ln("Z1c", c), pb(c, 0, 96))
-            for k in range(3 * c, 3 * c + 3):
-                cs = s_[:, 512 * k:512 * k + 512]
-                fb = ap("F%d" % (k % PAR["nb"]))
-                tt(ap(hh, cs), ind(ap("Wn", s_[:, 0:4 * NW if st > 1 else NW]), ap("u1", s_[:, 32 * k:32 * k + 32])), ap("ga", cs), A.add)
-                twice = cons and (st, k) in PAR["fs"]
-                terms = [(fb, ap("Ib"), ap("fb", cs))] + [(fb, ap("Ic"), ap(x, cs)) for x in held]
-                mm(grp(terms + ([(fb, ap("big", s_[0:1, :]), ap("oneb", s_[0:1, :]))] if cons and not twice else [])))
-                act(ap("qq", cs), fb, AF.Identity, -127.5 if cons and not twice else 49024.5)
-                if twice:
-                    mm(grp(terms + [(fb, ap("nIb"), ap("qq", cs))]))
-                    act(ap("fb", cs), fb, AF.Identity, 49152.0)
-                elif cons:
-                    tt(ap("fb", cs), fb, ap("qq", cs), A.subtract)
-                if st == NST:
-                    dma(ap("yf", cs), ap("fb", cs))
-            nf = 8 if st == NST else 16
-            mm([(pb(c, i, 16 * nf, 96, 16), im(hh, c, i), ap("Wh", s_[:, 0:nf]), True, True) for i in range(16)])
-            act(lm("Zb", c), pb(c, 0, 128, 96))
-            if st < NST:
-                tt(lm("Aa", c), pb(c, 128, 256, 96), lm("Aa", c), A.add)
-            mm(grp([(pb(c, 128, 224), lm("Zb", c), ap("I32", s_[0:96, 0:96])), (pb(c, 128, 224), ap("nI32"), ln("Z1c", c)),
-                    (pb(c, 128, 224), ap("nS0"), ln(En, c))]))
-            ts(ln("bt", c), pb(c, 128, 224), OFF, None, A.add)
-            ts(ln("b32", c), ln("bt", c), NW - 1, None, A.bitwise_and)
-            if st < NST:
-                copy(ln("b16", c), ln("b32", c))
-                mm([(pb(c, i, 128, 96, 16), im("qq", c, i), ap("Wq"), True, True) for i in range(16)])
-            else:
-                copy(ln("yi", c), ln("b32", c))
-                dma(ln("yimg", c), ln("yi", c))
-        tag[0] = "c"
-        if cons:
-            held = []
-        X = qb(0, 256, 448)
-        mm([(X, ap("Dm"), ap("FL"), True, False), (X, ap("Ic"), ap("JC"), False, False)]
-           + [(qb(0, 256 + k, 448, 128, 16), ap("EX", s_[:, 128 * k:128 * k + 128]), ap(mo), False, k == 15) for k in range(16)])
-        ts(ap("Rr"), X, cc(11), cc(12), A.mult, A.add)
-        for o in (0, 1):
-            ts(ap("Lm", s_[:, :, 16 * o:16 * o + 16]), X, cc(13 + 2 * o), cc(14 + 2 * o), A.mult, A.add)
-        mm(grp([(qb(1, 256, 448), ap("Sel01"), ap(Ep)), (qb(1, 256, 448), ap("Sel11"), ap("Rr"))]))
-        act(ap("SRC", s_[:, 0:NK]), qb(1, 256, 448), AF.Identity, cc(5))
-        for k in range(12):
-            a, cb = k // 3, k % 3
-            D = qb(k % 3, 0, 192)
-            mm([(D, ap("Lm", s_[32 * a:32 * a + 32, 4 * cb:4 * cb + 4, :]), ap("Rr", s_[32 * a:32 * a + 32, :]), True, True)])
-            act(ap("junk", s_[:, 192 * (k % 2):192 * (k % 2) + 192]), D, AF.Relu, 0.0, -1.0, ap("acc", s_[:, k:k + 1]))
-        Y = qb(1, 448, 460)
-        mm(grp(diag("BigL", lambda k: ap(En, s_[:, k::16]), Y) + [(Y, ap("nIc"), ap(mo))]))
-        ts(ap("t1"), Y, 0.0, 8192.0, A.is_le, A.mult)
-        tt(ap("t1"), ap("t1"), ap("wf"), A.add)
-        if st < NST:
-            tt(ap("t2"), Y, ap("wf"), A.add)
-        tt(ap("flag"), ind(ap("acc"), ap("o4", s_[:, 0:3])), ap("TH"), A.is_gt)
-        Y = qb(1, 464, 476)
-        mm(grp([(Y, ap("I32"), ap("t1"))]
-               + [(Y, ap("Fold", s_[:, 96 - 32 * a:224 - 32 * a]), ap("flag", s_[:, 12 * a:12 * a + 12])) for a in range(4)]))
-        tt(ap("SRC", s_[:, NK:]), Y, ap("dum"), A.min)
-        if st < NST:
-            tt(ap("t3"), ap("t2"), Y, A.subtract)
-            ts(ap("t3"), ap("t3"), 0.0, 2.0, A.max, A.add)
-            tt(ap(mn), ap("t3"), ap(mo), A.add)
-        src, tb = "SRC", TB
-        if st % NEV == 0:
-            src, tb = "RD%d" % st, ("TB2" if st == NEV else "TB3")
-            remote(ap(src, s_[:, 0:NK]), ap("SRC", s_[:, 0:NK]))
-            remote(ap(src, s_[:, NK:]), ap("SRC", s_[:, NK:]))
-        copy(ap("off"), ap(src, s_[:, NK:]))
-        copy(ind(ap(tb), ap("off")), ap(src, s_[:, 0:NK]))
-        if st % NEV == NEV - 1:
-            cm, rc, nb = ("CM1", "RC1", "TB2") if st < NEV else ("CM2", "RC2", "TB3")
-            for k in range(3):
-                dma(ap(cm, s_[:, 128 * k:128 * k + 128]), ap(TB, s_[TROW[k]::16, 0:NW]))
-            remote(ap(rc), ap(cm))
-            if st < NEV:
-                copy(ap("RF1"), ap(rc))
-                rc = "RF1"
-            for k in range(3):
-                dma(ap(nb, s_[TROW[k]::16, 0:NW]), ap(rc, s_[:, 128 * k:128 * k + 128]))
+        for part, cs in ((choose, (0, 1)), (winners, (2,)), (letters, (0, 1))):
+            for c in cs:
+                tag[0] = c
+                part(st, c) if c < 2 else part(st)
     for k, o in enumerate((ap("yent", s_[:, 0:NW]), ap("yent", s_[:, NW:]), ap("yelen"))):
         dma(o, ap("TB3", s_[TROW[k]::16, 0:NW]))
+    for e, names in PAR["first"].items():
+        mine, last = [i for i, o in enumerate(ops) if o["eng"] == e and o["st"] == 0], None
+        for nm in [x.split("*")[0] for x in names.split() for _ in range(int((x + "*1").split("*")[1]))]:
+            if nm == "|":
+                gate = last
+                continue
+            i = [i for i in mine if ops[i]["wr"][0][0] == nm][0]
+            mine.remove(i)
+            ops[i]["after"], last = last, i
+        for i in mine:
+            ops[i]["after"] = gate
     return ops
 
 
@@ -409,16 +509,205 @@ def link(ops):
                     if (w or mine) and bx[2] <= b2[3] and b2[2] <= bx[3] and not bx[1].isdisjoint(b2[1]):
                         d[j] = d.get(j, False) or w
         o["dep"] = d
-        o["banks"] = sorted(set(b[0] for b in o["rd"] + o["wr"] if b[0] in SCRATCH and SCRATCH[b[0]][0] == "psum"))
-        for w, lst in ((False, o["rd"]), (True, o["wr"])):
+        o["banks"] = sorted(set((b[0], k) for b in o["rd"] + o["wr"] if b[0] in SCRATCH and SCRATCH[b[0]][0] == "psum"
+                                for k in range(b[2] // 512, b[3] // 512 + 1)))
+        for w, lst in ((False, set(o["rd"])), (True, set(o["wr"]))):
             for bx in lst:
                 hist.setdefault(bx[0], []).append((i, w, bx))
+
+
+def span(o):
+    k, a = o["kind"], o["args"]
+    size = {F32: 4, I32: 4, BF: 2, F16: 2, U16: 2}
+    if k == "mm":
+        t = sum(max(min(64, _box(l)[4]), _box(r)[4]) * (1.68 if _dt(l[0]) == F32 else 0.42) for (_, l, r, _, _) in a)
+        return t, t + 100
+    n = o["wr"][0][4]
+    if k in ("dma", "rem"):
+        by = n * len(o["wr"][0][1]) * size[_dt(a[1][0])]
+        return (60, 1900 + by / 300, by / 300) if k == "dma" else (400, 2500 + by / 64, by / 128)
+    if len(a[0]) == 3:
+        t = 50 + 0.83 * 3 * _box(a[1])[4]
+    elif isinstance(a[1], tuple) and len(a[1]) == 3:
+        t = 60 + 0.83 * (max(2, PAR["ga"]) if k == "tt" else PAR["ga"]) * n
+    elif o["eng"] == "G":
+        t = 150 + 1.66 * n
+    elif o["eng"] == "S":
+        t = 65 + 0.83 * n + (20 if a[5] else 0)
+    else:
+        wide = [b for b in o["rd"] + o["wr"] if b[4] == n]
+        psum = any(SCRATCH[b[0]][0] == "psum" for b in wide)
+        rate = (1 if psum else 2) if k == "tt" else 0.5 if all(size[_dt(b[0])] == 2 for b in wide) else 1
+        t = 30 + 0.83 * max(64, n * rate)
+    return t, t
+
+
+def schedule(ops):
+    n, wake = len(ops), 60
+    sp = [tuple(int(x) for x in span(o)) for o in ops]
+    pred = [[(j, sp[j][0] if ops[j]["eng"] == "P" == o["eng"] and not o.get("fence") else sp[j][1] + (PAR["gwake"] if o["eng"] == "G" else wake))
+             for j in o["dep"]] for o in ops]
+    succ = [[] for _ in ops]
+    for i, o in enumerate(ops):
+        if o.get("after") is not None:
+            pred[i].append((o["after"], sp[o["after"]][0]))
+    topo, seen = [], set()
+
+    def visit(i):
+        if i not in seen:
+            seen.add(i)
+            for (j, lag) in pred[i]:
+                visit(j)
+            topo.append(i)
+    for i in range(n):
+        visit(i)
+    for i in range(n):
+        for (j, lag) in pred[i]:
+            succ[j].append((i, lag))
+    uses = [[(o["eng"], sp[i][0], None)] + [(b, sp[i][1] + wake, o["eng"]) for b in o["banks"]] for i, o in enumerate(ops)]
+
+    def place(order, back):
+        at, busy = [0] * n, {}
+        for i in order:
+            t = max([at[k] + lag for (k, lag) in succ[i]] + [sp[i][1]]) if back else max([at[j] + lag for (j, lag) in pred[i]], default=0)
+            moved = True
+            while moved:
+                moved = False
+                for (res, d, e) in uses[i]:
+                    lo = t - d if back else t
+                    lst = busy.get(res, ())
+                    k = len(lst)
+                    while k and lst[k - 1][0] > lo - 4000:
+                        k -= 1
+                    for (a, b, e2) in lst[k:]:
+                        if a >= lo + d:
+                            break
+                        if lo < b and (e is None or e != e2):
+                            t += b - lo
+                            lo, moved = b, True
+            at[i] = t
+            for (res, d, e) in uses[i]:
+                lst = busy.setdefault(res, [])
+                lo = t - d if back else t
+                k = len(lst)
+                while k and lst[k - 1][0] > lo:
+                    k -= 1
+                lst.insert(k, (lo, lo + d, e))
+        return at
+    lead = [PAR["lead"].get(o["name"], 0) for o in ops]
+    way = [0] * n
+    for i in reversed(topo):
+        way[i] = max([way[k] + lag for (k, lag) in succ[i]] + [sp[i][1]])
+        if ops[i]["name"] in ("VMx0.0", "VMx1.0") and PAR["beat"]:
+            beat, behind, tail = PAR["beat"]
+            way[i] = max(way[i], tail + beat * (NST - ops[i]["st"]) + behind * (ops[i]["name"] == "VMx0.0"))
+    best = None
+    rng = np.random.default_rng(PAR.get("seed", 1))
+    for _ in range(PAR["rounds"]):
+        for i in reversed(topo):
+            way[i] = max([way[k] + 1 for (k, lag) in succ[i]] + [way[i] + lead[i]])
+        at = place(sorted(range(n), key=lambda i: (-way[i], i)), False)
+        end = max(at[i] + sp[i][1] for i in range(n))
+        if best is None or end <= best[0]:
+            best = (end, at)
+        rnd = [int(x) for x in rng.integers(0, PAR["noise"] + 1, n)]
+        fin = [0] * n
+        for i in topo:
+            fin[i] = max([best[1][i] + sp[i][1] + rnd[i]] + [fin[j] + 1 for (j, lag) in pred[i]])
+        way = place(sorted(range(n), key=lambda i: (-fin[i], -i)), True)
+    return polish(ops, sp, sorted(topo, key=lambda i: best[1][i]))
+
+
+def polish(ops, sp, order):
+    n, wake = len(ops), 60
+    engs = sorted(set(o["eng"] for o in ops))
+    banks = sorted(set(b for o in ops for b in o["banks"]))
+    eng = [engs.index(o["eng"]) for o in ops]
+    bk = [[banks.index(b) for b in o["banks"]] for o in ops]
+    dep = [list(o["dep"]) + ([] if o.get("after") is None else [o["after"]]) for o in ops]
+    data = [[j for j in o["dep"] if not (ops[j]["eng"] == "P" == o["eng"] and not o.get("fence"))] for o in ops]
+    deps = [set(d) for d in dep]
+    wakes = [PAR["gwake"] if e == "G" else wake for e in engs]
+
+    def run(order):
+        done, why = [0] * n, [None] * n
+        free, last, turn, dma = [0] * len(engs), [None] * len(engs), [{} for _ in banks], 0
+        for i in order:
+            e = eng[i]
+            t, w = free[e], (last[e], True)
+            wk = wakes[e]
+            for j in data[i]:
+                if done[j] + wk > t:
+                    t, w = done[j] + wk, (j, False)
+            for b in bk[i]:
+                for e2, j in turn[b].items():
+                    if e2 != e and done[j] + wake > t:
+                        t, w = done[j] + wake, (j, j not in deps[i])
+                turn[b][e] = i
+            s = sp[i]
+            free[e], last[e], why[i] = t + s[0], i, w
+            if len(s) == 2:
+                done[i] = t + s[1]
+            else:
+                if dma > t + s[0] + 900:
+                    why[i] = (lastd, True)
+                dma, lastd = max(dma, t + s[0] + 900) + s[2], i
+                done[i] = dma + s[1] - s[2] - 900
+        return max(done) + sum(done) * PAR["pull"] / n, done, why
+    rng = np.random.default_rng(2)
+    cur = run(order)
+    best = (cur[0], order, max(cur[1]))
+    for it in range(PAR["swaps"]):
+        done, why = cur[1], cur[2]
+        u = rng.random(6)
+        i = done.index(max(done)) if u[0] < 0.5 else order[int(u[1] * n)]
+        held = []
+        while i is not None:
+            j, res = why[i]
+            if res and j is not None:
+                held.append((j, i))
+            i = j
+        if not held:
+            continue
+        j, i = held[int(u[2] * len(held))]
+        a, b = order.index(j), order.index(i)
+        if u[4] < 0.5:
+            if it % 2:
+                a = max(0, a - int(u[5] * PAR["jump"]))
+                j = order[a]
+            else:
+                b = min(n - 1, b + int(u[5] * PAR["jump"]))
+                i = order[b]
+        seg = order[a:b + 1]
+        if it % 2:
+            grp = {i}
+            for x in reversed(seg[:-1]):
+                if any(x in deps[y] for y in grp):
+                    grp.add(x)
+            new = [x for x in seg if x in grp] + [x for x in seg if x not in grp]
+        else:
+            grp = {j}
+            for x in seg[1:]:
+                if not deps[x].isdisjoint(grp):
+                    grp.add(x)
+            new = [x for x in seg if x not in grp] + [x for x in seg if x in grp]
+        if i in grp and j in grp:
+            continue
+        cand = order[:a] + new + order[b + 1:]
+        res = run(cand)
+        heat = PAR["heat"] * (1 - it / PAR["swaps"])
+        if res[0] <= cur[0] - heat * np.log(1 - u[3]):
+            order, cur = cand, res
+            if res[0] < best[0]:
+                best = (res[0], cand, max(res[1]))
+    PAR["est"] = best[2]
+    return best[1]
 
 
 def plan():
     ops = build()
     link(ops)
-    order = [(ord(ORDER[2 * k]) - 48) * 64 + ord(ORDER[2 * k + 1]) - 48 for k in range(len(ORDER) // 2)]
+    order = schedule(ops)
     cnt, nd, nr, bank = {}, 0, 0, {}
     for i in order:
         o = ops[i]
@@ -479,7 +768,7 @@ def rank_program(g, core, T, topo):
                 sem, val = ("r%d" % p["sig"], n_in) if w else ("l%d" % p["sig"], n_out)
             else:
                 sem, val = p["sig"]
-            if e == "P" and sem == "sP":
+            if e == "P" and sem == "sP" and not o.get("fence"):
                 continue
             need[sem] = max(need.get(sem, 0), val)
         for sem in sorted(need):

import numpy as np
from concourse.mybir import AluOpType as A, ActivationFunctionType as AF

NW, NK, NST, NEV = 2048, 192, 6, 3
TBW = NW + NK
F32, BF, F16, I32, U16 = "float32", "bfloat16", "float16", "int32", "uint16"
NCC = 10
SCRATCH = {}


def _sb(dtype, **kw):
    for k, n in kw.items():
        SCRATCH[k] = ("sbuf", [128] + (n if isinstance(n, list) else [n]), dtype)


_sb(BF, tw=NW, Wn=4 * NW, qq=3072, fo=3072, junk=400, ge=288, nI1=96, flag=12, onec=128, zerc=128, Ib=128, nIb=128, BO=128, BigZ=144,
    Big1=144, Wh=16, Wq=8, S0=128, S10=128, nS0=128, nS1=128, BP=128, YT=128, TN=512, npw=128, DW=[8, 16], SelL=128, SelM=128,
    Sel01=128, Sel11=128, SelJ=128, JC=NK, neg2=NK, mid=NK, Fold=128, high=128, ones=512)
_sb(F16, X=3072, Y=3072, FD=3072, tnh=512, FLW=NW, b16=NK, Am=NK, E0=NK, E1=NK, FL=NK, mf=NK, Rr=194, Lm=[12, 32], wf=12)
_sb(I32, tni=512, b32=NK, bt=NK, owi=NK, o15i=8, CI=384)
_sb(U16, u0=NK, u1=NK, wO=12, off=16, o15=8)
_sb(F32, TB1=TBW, TB2=TBW, TB3=TBW, Z1c=NK, ZS0=512, ZS1=512, Mx=256, Ml=16, acc=12 * 193, rsd=386, off32=12, SRC=NK, SR2=NK, CF=384,
    CM1=384, RC1=384, CM2=384, RC2=384, I32=128, nI32=128, nMV=96, segm=128, rst=128, pw=128, d0=128, d1=128, two=16, zer=16,
    VR=[NCC, 2, 16], CC=32 * NCC, dum=12, dumr=12, yi=NK, TH=12)
for _b in ("A0", "A1", "B0", "B1", "D0", "D1"):
    SCRATCH[_b] = ("psum", [128, 512], F32)
SCRATCH["FF"] = ("psum", [128, 1024], F32)
for _k in range(1, NST + 1):
    _sb(F32, **{"RD%d" % _k: NK})
    _sb(U16, **{"RO%d" % _k: 16})
NDS, NRS = 60, 14
SEMAPHORES = ["sV", "sS", "sP", "sG"] + ["d%d" % i for i in range(NDS)] + ["r%d" % i for i in range(NRS)] + ["l%d" % i for i in range(NRS)]
HBM = {"turn": [8, NW], "twist": [128, NW], "img": [128, NK], "ent": [8, 2 * NW], "elen": [8, NW], "own": [8, 2 * NK],
       "olen": [8, NK], "yimg": [128, NK], "yf": [128, 3072], "yent": [8, 2 * NW], "yelen": [8, NW]}
s_ = np.s_
PAR = {"pieces": ((0, 48, "S"), (48, 96, "V")), "raw": {4: ((0, 48, "S"), (48, 96, "T")), 6: ((0, 48, "S"), (48, 96, "U"))}, "whole": True, "q": ((0, 48, "V"), (48, 96, "V")), "ev": "SSS", "zp": ((0, 96),),
       "mod1": (True, True), "init": ((0, 48, "S"), (48, 96, "V")), "ahead": (1, 1), "gc": 2, "tb": 1200, "last": "SV",
       "eng": {"Ml": "V", "E": "S", "bt": "S", "b16": "S", "FL": "S", "Rr": "S", "Lm": "SS", "SRC": "S", "D": "SSSVVV", "b0": "S", "dump": "S", "mf": "S", "E0": "S"}, "pairs": (0, 3, 1, 4, 2, 5),
       "beat": None, "gwake": 900, "swaps": 15000, "jump": 30, "heat": 300, "pull": 3, "rounds": 20, "noise": 1000, "ga": 1.5, "lead": {},
       "first": {"Y": "b32 tw CI*3 owi*3 TB1*3 Wn*6 |", "S": "tni tw | npw TN*4 Wh*2 YT",
                 "V": "onec zerc DW d0*2 d1*2 pw owi two zer VR*3 CC tnh TN | BP TB1",
                 "G": "o15i ge JC dumr BO Ib DW S0 BO TN DW TN*3 TB1 |"}}


def _shape(name):
    return SCRATCH[name][1] if name in SCRATCH else HBM[name]


def _dt(name):
    return SCRATCH[name][2] if name in SCRATCH else F32


def _box(x):
    name, idx = x[0], x[1]
    sh = _shape(name)
    idx = idx if isinstance(idx, tuple) else (idx,)
    idx = list(idx) + [slice(None)] * (len(sh) - len(idx))
    rs = [range(sh[d])[i] if isinstance(i, slice) else range(i, i + 1) for d, i in enumerate(idx)]
    lo = hi = 0
    n = 1
    for d in range(1, len(sh)):
        lo, hi, n = lo * sh[d] + rs[d][0], hi * sh[d] + rs[d][-1], n * len(rs[d])
    return (name, frozenset(rs[0]), lo, hi, n)


def ap(name, idx=slice(None)):
    return (name, idx)


def ind(win, offs):
    return (win[0], win[1], offs)


def build():
    ops = []
    tag, seen = [3, 0], {}
    ENG = PAR["eng"]

    def add(eng, kind, args, reads, writes):
        rd, wr = [], []
        for x in reads:
            if isinstance(x, tuple):
                rd.append(_box(x))
                if len(x) == 3:
                    rd.append(_box(x[2]))
        for x in writes:
            wr.append(_box(x))
            if len(x) == 3:
                rd.append(_box(x[2]))
        name = "%s%s%s" % (eng, wr[0][0].rstrip("0123456"), tag[0])
        seen[(name, tag[1])] = seen.get((name, tag[1]), -1) + 1
        ops.append(dict(eng=eng, kind=kind, args=args, rd=rd, wr=wr, st=tag[1], name=name + "." + str(seen[(name, tag[1])])))

    def copy(out, in_):
        add("V", "copy", (out, in_), [in_], [out])

    def ts(out, in_, a, b, o0, o1=None):
        add("V", "ts", (out, in_, a, b, o0, o1), [in_, a, b], [out])

    def tt(out, x, y, o):
        add("V", "tt", (out, x, y, o), [x, y], [out])

    def mset(out, v):
        add("V", "mset", (out, v), [], [out])

    def scan(out, x, y, init, o0, o1):
        add("V", "scan", (out, x, y, init, o0, o1), [x, y], [out])

    def turn32(out, in_):
        add("V", "vtr", (out, in_), [in_], [out])

    def act(out, in_, func=AF.Identity, bias=0.0, scale=1.0, accum=None):
        add("S", "act", (out, in_, func, bias, scale, accum), [in_, bias, scale], [out] + ([accum] if accum else []))

    def iota(out, pat, base, cm=0):
        add("G", "iota", (out, pat, base, cm), [], [out])

    def asel(out, in_, pat, cmp, fill, base, cm):
        add("G", "asel", (out, in_, pat, cmp, fill, base, cm), [in_], [out])

    def lin(e, out, in_, bias=0.0, scale=1.0):
        if e == "G":
            asel(out, in_, [[0, _box(out)[4]]], A.is_ge, 0.0, 0, 0)
        elif e == "S":
            act(out, in_, AF.Identity, bias, scale)
        elif scale == 1.0 and bias == 0.0:
            copy(out, in_)
        elif scale == 1.0:
            ts(out, in_, bias, None, A.add)
        else:
            ts(out, in_, scale, bias, A.mult, A.add)

    def mm(*parts, each=False):
        parts = [x for x in parts if x]
        for n, items in enumerate(parts):
            lst = [(o, l, r, each or k == 0 == n, each or (k == len(items) - 1 and n == len(parts) - 1)) for k, (o, l, r) in enumerate(items)]
            add("P", "mm", lst, [x[1] for x in lst] + [x[2] for x in lst], [x[0] for x in lst])
            k = _box(lst[0][0])[2] // 512
            ops[-1]["wr"].append(("turn of " + lst[0][0][0], frozenset([0]), k, k, 0))

    def dma(out, in_, q="Y"):
        add(q, "dma", (out, in_), [in_], [out])

    def remote(out, in_):
        add("G", "rem", (out, in_), [in_], [out])

    def cc(k):
        return ap("CC", s_[:, 32 * k:32 * k + 1])

    TROW = (0, 1, 11)
    QB = 49152.0

    dma(ap("tw", s_[:, 0:1024]), ap("twist", s_[:, 0:1024]))
    dma(ap("tw", s_[:, 1024:2048]), ap("twist", s_[:, 1024:2048]), "S")
    dma(ap("b32"), ap("img"))
    dma(ap("tni", s_[0:32, :]), ap("turn"), "S")
    mset(ap("owi"), 0)
    for k, (src, osrc) in enumerate(((ap("ent", s_[:, 0:NW]), ap("own", s_[:, 0:NK])), (ap("ent", s_[:, NW:]), ap("own", s_[:, NK:])),
                                     (ap("elen"), ap("olen")))):
        dma(ap("CI", s_[:, 128 * k:128 * k + 128]), src)
        dma(ap("owi", s_[TROW[k]::16, :]), osrc)
    mset(ap("TB1", s_[:, PAR["tb"]:]), 0.0)
    iota(ap("TB1", s_[:, 0:PAR["tb"]]), [[0, PAR["tb"]]], 0)
    lin("S", ap("CF", s_[:, 0:256]), ap("CI", s_[:, 0:256]))
    lin("S", ap("CF", s_[:, 256:]), ap("CI", s_[:, 256:]), -2048.0)
    for k in range(3):
        dma(ap("TB1", s_[TROW[k]::16, 0:NW]), ap("CF", s_[:, 128 * k:128 * k + 128]))

    mset(ap("onec"), 1.0)
    mset(ap("zerc"), 0.0)
    asel(ap("Ib"), ap("onec"), [[-1, 128]], A.is_equal, 0.0, 0, 1)
    asel(ap("BO"), ap("onec"), [[-16, 8], [0, 16]], A.is_ge, 0.0, 0, 1)
    asel(ap("BO"), ap("BO"), [[16, 8], [0, 16]], A.is_ge, 0.0, 15, -1)
    for nm, v, v0 in (("d0", 0.5, 0.0), ("d1", 0.0, 1.0)):
        mset(ap(nm), v)
        mset(ap(nm, s_[:, 0::16]), v0)
    lin("S", ap("rst"), ap("d1"), 0.0, -2.0 ** 22)
    scan(ap("pw"), ap("d0"), ap("d1"), 0.0, A.mult, A.add)
    mset(ap("two"), 2.0)
    mset(ap("zer"), 0.0)
    mset(ap("VR"), 0.0)

    def vr(k, t0, t1, v, o=slice(None)):
        x = ap("VR", s_[:, k, o, t0:t1])
        if k < PAR["gc"]:
            mset(x, v)
        elif v == int(v):
            iota(x, [[0, _box(x)[4]]], int(v))
        else:
            asel(x, x, [[0, _box(x)[4]]], A.not_equal, v, 0, 0)
    for o in (0, 1):
        scan(ap("VR", s_[:, 0, o, 0:11]), ap("two", s_[:, 0:11]), ap("zer", s_[:, 0:11]), 2.0 ** -9, A.mult, A.add)
    turn32(ap("CC", s_[:, 0:32]), ap("VR", s_[:, 0]))
    ts(ap("VR", s_[:, 1]), ap("pw", s_[:, 0:32]), 0.5, 1535.5, A.mult, A.add)
    vr(1, 0, 1, 0.0); vr(1, 1, 2, 1023.75)
    bits = ((0, 2, 128 * 2048 - 64), (2, 11, 128 * 1536 - 64))
    vr(2, 0, 11, -0.5); vr(2, 11, 13, 1)
    for (t0, t1, v) in bits + ((11, 12, 2), (13, 15, 1)):
        vr(3, t0, t1, v)
    for o in (0, 1):
        vr(4 + 2 * o, 0, 11, -0.5, o); vr(4 + 2 * o, 13, 15, 1, o); vr(4 + 2 * o, 15, 16, -1, o)
        for (t0, t1, v) in bits + ((11, 13, -1), (13, 14, 2)):
            vr(5 + 2 * o, t0, t1, v, o)
    iota(ap("VR", s_[:, 8]), [[0, 2], [1, 16]], 0)
    vr(9, 11, 12, -45056); vr(9, 12, 13, -0.5); vr(9, 13, 14, 1); vr(9, 15, 16, 1)
    turn32(ap("CC", s_[:, 32:]), ap("VR", s_[:, 1:]))
    BM = ap("BO", s_[:, 0::16])
    lin("S", ap("I32"), ap("Ib")); lin("S", ap("nI32"), ap("Ib"), 0.0, -1.0)
    asel(ap("nIb"), ap("zerc"), [[-1, 128]], A.not_equal, -1.0, 0, 1)
    asel(ap("Fold"), ap("zerc"), [[-1, 128]], A.not_equal, 8192.0, 0, 1)
    for nm, col in (("BigZ", cc(0)), ("Big1", 1.0)):
        mset(ap(nm), 0.0)
        lin("S", ap(nm, s_[:, 15:143:16]), BM, 0.0, col)
    lin("S", ap("Wh", s_[:, 0:8]), BM, 0.0, cc(0)); lin("S", ap("Wh", s_[:, 8:16]), BM); lin("S", ap("Wq"), BM, 0.0, -1.0)
    tt(ap("BP"), ap("BO"), ap("pw"), A.mult)
    lin("S", ap("YT"), ap("BP"), 0.0, cc(0))
    lin("S", ap("npw", s_[0:32, :]), ap("pw", s_[0:32, :]), 0.0, -1.0)
    mset(ap("tnh", s_[32:64, :]), 1.0)
    mset(ap("TN", s_[32:64, :]), -0.5)
    for k in range(4):
        asel(ap("TN", s_[0:32, 128 * k:128 * k + 128]), ap("npw", s_[0:32, :]), [[-4, 8], [0, 16]], A.is_equal, 0.0, -k, 1)
        lin("S", ap("TN", s_[32:33, 128 * k:128 * k + 128]), ap("pw", s_[32:33, :]), 0.0, 2.0 ** -9)
    mset(ap("DW"), 0.0)
    for k, v in ((0, -256.0), (1, 512.0)):
        asel(ap("DW", s_[:, :, 0:11]), ap("DW", s_[:, :, 0:11]), [[-16, 8], [-1, 11]], A.not_equal, v, -k, 1)

    def link_rows(out, in_, t, t2, v):
        asel(ap(out), ap(in_), [[-16, 8], [0 if t2 is None else 128, 16]], A.not_equal, v, -t - 128 * (t2 or 0), 1)
    link_rows("S0", "zerc", 0, None, 1.0); link_rows("nS0", "zerc", 0, None, -1.0); link_rows("S10", "nS0", 1, None, 1.0)
    link_rows("nS1", "zerc", 1, None, -1.0)
    link_rows("SelL", "zerc", 11, 15, 1.0); link_rows("Sel11", "zerc", 11, 11, 1.0); link_rows("SelM", "Sel11", 11, 13, 1.0)
    link_rows("Sel01", "Ib", 11, 11, 0.0); link_rows("SelJ", "zerc", 0, 12, 1.0 / 256); link_rows("SelJ", "SelJ", 0, 14, 1.0 / 256)
    v0 = min(l0 for (l0, l1, t) in PAR["pieces"] if t == "V")
    asel(ap("nMV", s_[0:96, :]), ap("nI32", s_[0:96, 0:96]), [[1, 96]], A.is_ge, 0.0, -v0, 0)
    iota(ap("o15i"), [[1, 8]], 0)
    copy(ap("o15"), ap("o15i"))
    for c in range(2):
        lin("S", ap("Mx", s_[96:128, 128 * c:128 * c + 128]), ap("pw", s_[96:128, :]), 0.0, -1.0)
    iota(ap("ge", s_[:, 15::144]), [[0, 2]], 1)
    lin("S", ap("nI1", s_[0:96, :]), ap("Ib", s_[0:96, 0:96]), 0.0, -1.0)
    mset(ap("nI1", s_[96:97, :]), 1.0)
    iota(ap("JC"), [[1, NK]], 0)
    mset(ap("neg2"), -2.0)
    iota(ap("dumr"), [[16, 12]], NW)
    ts(ap("dum"), ap("dumr"), cc(8), None, A.add)
    mset(ap("off"), 0)
    lin("G", ap("Rr", s_[:, 192:193]), cc(9))
    if "V" in ENG["D"]:
        for e, n0, n1 in [(e, n, n + len(e)) for n, e in ((0, ENG["D"].rstrip("V")), (len(ENG["D"].rstrip("V")), ENG["D"].lstrip("S"))) if e]:
            iota(ap("TH", s_[:, 2 * n0:2 * n1]), [[0, 2 * (n1 - n0)]], 0 if e[0] == "S" else 45056)
        iota(ap("rsd"), [[0, 386]], 0)
        iota(ap("rsd", s_[:, 0::193]), [[0, 2]], -2 ** 22)
    for nm in ("TB2", "TB3"):
        for k in range(0, TBW, 560):
            iota(ap(nm, s_[:, k:k + 560]), [[0, 560]], 0)
    iota(ap("mid"), [[0, NK]], 2048)
    iota(ap("high", s_[0:32, :]), [[0, 128]], int(QB))
    iota(ap("ones", s_[0:32, :]), [[0, 512]], 1)

    copy(ap("tnh", s_[0:32, :]), ap("tni", s_[0:32, :]))
    MAG = 1.5 * 2 ** 23
    for k in range(4):
        cs = s_[:, 512 * k:512 * k + 512]
        yb = ap("FF", s_[:, 512 * (k % 2):512 * (k % 2) + 512])
        mm([(yb, ap("YT"), ap("tw", cs))], [(yb, ap("TN", s_[0:34, 128 * k:128 * k + 128]), ap("tnh", s_[0:34, :]))])
        ts(ap("FLW", cs), yb, MAG, MAG, A.add, A.subtract)
        wb = ap(("D0", "D1")[k % 2])
        mm([(wb, ap("Ib"), ap("tw", cs))], [(wb, ap("DW"), ap("FLW", cs))])
        act(ap("Wn", cs), wb)
        if k % 2:
            for n in (1, 2, 3):
                dma(ap("Wn", s_[:, n * NW + 512 * k - 512:n * NW + 512 * k + 512]), ap("Wn", s_[:, 512 * k - 512:512 * k + 512]))

    def ln(name, c, l0=0, l1=96):
        return ap(name, s_[:, 96 * c + l0:96 * c + l1])

    def big(name, c, l0, l1):
        return ap(name, s_[:, 1536 * c + 16 * l0:1536 * c + 16 * l1])

    def pa(c, a, b, p=128, st=None):
        return ap("A%d" % c, s_[0:p, a:b:st])

    def pb(c, a, b, p=128, st=None):
        return ap("B%d" % c, s_[0:p, a:b:st])

    def im(name, c, i, l0=0, l1=96):
        return ap(name, s_[:, 1536 * c + 16 * l0 + i:1536 * c + 16 * l1:16])

    def zs(n, c, a, b):
        return ap("ZS%d" % (n % 2), s_[0:96, 256 * c + a:256 * c + b])

    def diag(big_, rhs, out):
        return [(out, ap(big_, s_[:, 15 - k:143 - k]), rhs(k)) for k in range(16)]

    def turned(n, c, nf):
        mm([(pb(c, 96 + i, 96 + 16 * nf, 96, 16), im("X", c, i), ap("Wh", s_[:, 0:nf])) for i in range(16)], each=True)
        act(zs(n, c, 0, 16 * nf), pb(c, 96, 96 + 16 * nf, 96))

    nb = [0]

    def summed(c, l0, l1, terms, high=False, banks=None):
        nb[0] += 1
        name, k0 = banks or ("FF", 512 * (nb[0] % 2) if l1 - l0 <= 32 else 0)
        for l in range(l0, l1, 32):
            m = min(l + 32, l1)
            f = ap(name, s_[:, k0 + 16 * (l - l0):k0 + 16 * (m - l0)])
            lst = [(f, ap("high", s_[0:1, :]), ap("ones", s_[0:1, 0:16 * (m - l)]))] if high else []
            lst += [(f, ap(w), big(v, c, l, m)) for (w, v) in terms]
            mm(lst[:-1], lst[-1:])
        return ap(name, s_[:, k0:k0 + 16 * (l1 - l0)])

    def ahead(tb, cm, rc, nx):
        for k in range(3 if tb else 0):
            dma(ap(cm, s_[:, 128 * k:128 * k + 128]), ap(tb, s_[TROW[k]::16, 0:NW]))
        remote(ap(rc), ap(cm))
        if nx == "TB3":
            lin("S", ap(rc, s_[:, 256:]), ap(rc, s_[:, 256:]), 2048.0)
        for k in range(3):
            dma(ap(nx, s_[TROW[k]::16, 0:NW]), ap(rc, s_[:, 128 * k:128 * k + 128]))

    lin(ENG["E0"], ap("E0"), ap("owi"))
    lin("S", ap("mf"), ap("owi"), -2048.0)
    copy(ap("u1"), ap("b32"))
    lin(ENG["b0"], ap("b16"), ap("b32"))
    for c in range(2):
        for (l0, l1, e) in PAR["init"]:
            lin(e, big("X", c, l0, l1), ind(ap("tw"), ln("u1", c, l0, l1)))
        turned(0, c, 16)
    if PAR["ahead"][0] == 0:
        ahead(None, "CF", "RC1", "TB2")

    OFF = 4096 - 127.5 / 256

    def choose(st, c):
        TB, En = "TB1" if st <= NEV else "TB2", "E%d" % (st % 2)
        mx = ap("Mx", s_[:, 128 * c:128 * c + 128])
        K = zs(0, c, 128, 256) if st == 1 else pb(c, 352, 480, 96)
        scan(ap("Mx", s_[0:96, 128 * c:128 * c + 128]), ap("rst", s_[0:96, :]), K, 0.0, A.add, A.max)
        g0 = 144 * c + 16
        ml = ap("Ml", s_[:, 8 * c:8 * c + 8])
        lin(ENG["Ml"], ml, ap("Mx", s_[:, 128 * c + 15:128 * c + 128:16]))
        tt(ap("ge", s_[:, g0:g0 + 128]), ind(ml, ap("o15")), mx, A.is_equal)
        mm([(pa(c, 128, 224), ap("ge", s_[0:96, g0:g0 + 128]), ap("Ib", s_[0:96, 0:96])),
            (pa(c, 128, 224), ap("ge", s_[0:97, g0 - 1:g0 + 127]), ap("nI1", s_[0:97, :]))])
        tt(ln("Am", c), pa(c, 128, 224), ln("b32", c), A.mult)
        mm(diag("Big1", lambda k: ap("Am", s_[:, 96 * c + k:96 * c + 96:16]), pa(c, 224, 230)))
        wo = ap("wO", s_[:, 6 * c:6 * c + 6])
        copy(wo, pa(c, 224, 230))
        lin(ENG["E"], ln(En, c), ind(ap(TB, s_[:, 0:NW]), wo))
        act(ap("wf", s_[:, 6 * c:6 * c + 6]), pa(c, 224, 230))
        mm([(pa(c, 256, 352), ap("Ib"), ln("b16", c))], [(pa(c, 256, 352), ap("S0"), ln(En, c))])
        if st == 1 and PAR["mod1"][0]:
            copy(ln("bt", c), pa(c, 256, 352))
            ts(ln("bt", c), ln("bt", c), NW - 1, None, A.bitwise_and)
            copy(ln("u0", c), ln("bt", c))
        else:
            copy(ln("u0", c), pa(c, 256, 352))

    def letters(st, c):
        En = "E%d" % (st % 2)
        raw = st in PAR["raw"]
        pieces = PAR["raw"][st] if raw else PAR["pieces"]
        kept = [l0 for (l0, l1, t) in pieces if t in "VWT"]
        w0 = ap("Wn", s_[:, 0:NW if st == 1 and PAR["mod1"][0] else 2 * NW])
        w1 = ap("Wn", s_[:, 0:NW if st == 1 and PAR["mod1"][1] else 4 * NW])
        for (l0, l1, t) in pieces:
            if t in "VWT":
                tt(big("Y", c, l0, l1), ind(w0, ln("u0", c, l0, l1)), big("X", c, l0, l1), A.add)
            else:
                lin("V" if t in "QU" else "S", big("Y", c, l0, l1), ind(w0, ln("u0", c, l0, l1)))
        for (l0, l1) in PAR["zp"]:
            z = pb(c, l0, l1)
            old = [] if not kept or l1 <= v0 else [(z, zs(st - 1, c, 0, 128), ap("nMV", s_[0:96, l0:l1]))]
            mm(old + [(z, ap("S10"), ln(En, c, l0, l1))], diag("BigZ", lambda i: im("Y", c, i, l0, l1), z))
            if st == 1 and PAR["mod1"][1]:
                ts(ln("bt", c, l0, l1), z, OFF, None, A.add)
                ts(ln("bt", c, l0, l1), ln("bt", c, l0, l1), NW - 1, None, A.bitwise_and)
                copy(ln("u1", c, l0, l1), ln("bt", c, l0, l1))
            else:
                ts(ln("u1", c, l0, l1), z, OFF, None, A.add)
        if not raw:
            act(ln("Z1c", c), pb(c, 0, 96))
        for p, (l0, l1, t) in enumerate(pieces):
            x, y, q, fd = (big(nm, c, l0, l1) for nm in ("X", "Y", "qq", "FD"))
            if t == "V":
                tt(x, ind(w1, ln("u1", c, l0, l1)), y, A.add)
                continue
            lin("V" if t in "RUT" else "S", fd, ind(w1, ln("u1", c, l0, l1)))
            terms = ([] if t in "WT" else [("Ib", "X")]) + ([("nIb", "qq")] if st == NEV + 1 else []) + [("Ib", "Y"), ("Ib", "FD")]
            if st < NST:
                for (l, m) in ((l0, l1),) if PAR["whole"] else [(l, min(l + 32, l1)) for l in range(l0, l1, 32)]:
                    lin(PAR["ev"][p], big("X", c, l, m), summed(c, l, m, terms), QB if st == NEV + 1 else 0.0)
                continue
            for n, l in enumerate(range(l0, l1, 32)):
                m = min(l + 32, l1)
                f = summed(c, l, m, terms, True, (("B%d" % c, 0), None)[(n + p) % 2])
                lin(PAR["last"][0], big("qq", c, l, m), f, -127.5)
                tt(big("fo", c, l, m), f, big("qq", c, l, m), A.subtract)
            dma(big("yf", c, l0, l1), big("fo", c, l0, l1))
        z = pa(c, 352, 448)
        if st < NST:
            for (l0, l1, e) in PAR["q"]:
                lin(e, big("qq", c, l0, l1), big("X", c, l0, l1), QB - 127.5)
            turned(st, c, 16)
        if raw:
            mm([(z, ap("nS1"), ln(En, c))], diag("BigZ", lambda i: im("FD", c, i), z))
        else:
            mm([(z, zs(st - 1, c, 0, 128), ap("nI32", s_[0:96, 0:96])), (z, ap("nI32"), ln("Z1c", c)), (z, ap("nS0"), ln(En, c))],
               [(z, zs(st, c, 0, 128), ap("I32", s_[0:96, 0:96]))])
        lin(ENG["bt"], ln("bt", c), z, OFF)
        ts(ln("b32", c), ln("bt", c), NW - 1, None, A.bitwise_and)
        if st < NST:
            mm([(pb(c, 352, 480, 96), ap("I32", s_[0:96, 0:96]), zs(st, c, 128, 256))],
               [(pb(c, 352 + i, 480, 96, 16), im("qq", c, i), ap("Wq")) for i in range(16)])
            lin(ENG["b16"], ln("b16", c), ln("b32", c))
        else:
            lin("S", ln("yi", c), ln("b32", c))
            dma(ln("yimg", c), ln("yi", c))

    def winners(st):
        ep = (st - 1) // NEV
        TB, NX, En, Ep = "TB%d" % (ep + 1), "TB%d" % (ep + 2), "E%d" % (st % 2), "E%d" % (1 - st % 2)
        Xb = ap("D0", s_[:, 0:192])
        mm([(ap("D1", s_[:, 0:192]), ap("BP"), ap("Am"))])
        lin(ENG["FL"], ap("FL"), ap("D1", s_[:, 0:192]), cc(1))
        mm([(Xb, ap("SelM"), ap("mf")), (Xb, ap("SelJ"), ap("JC"))] + ([(Xb, ap("SelM"), ap("neg2"))] if st == 1 else []),
           [(Xb, ap("SelL"), ap(En))], [(Xb, ap("DW"), ap("FL"))])
        lin(ENG["Rr"], ap("Rr", s_[:, 0:192]), Xb, cc(3), cc(2))
        for o in (0, 1):
            lin(ENG["Lm"][o], ap("Lm", s_[:, :, 16 * o:16 * o + 16]), Xb, cc(5 + 2 * o), cc(4 + 2 * o))
        dump = ap(TB, s_[:, NW:])
        sent = (st - 1) % NEV >= PAR["ahead"][ep]
        Sb = ap("D1", s_[:, 200:392])
        words = [(Sb, ap("Sel01"), ap(Ep)), (Sb, ap("Sel11"), ap("Rr", s_[:, 0:192]))]
        if st < NST:
            lin(ENG["dump"], dump, ap(En))
            mm(words)
            lin(ENG["SRC"], ap("SRC"), Sb)
        if sent and ep == 1:
            mm([(Sb, ap("Sel11"), ap("mid"))] + words)
            lin(ENG["SRC"], ap("SR2"), Sb)
        if sent:
            remote(ap("RD%d" % st), ap(("SRC", "SR2")[ep]))
        for u, n in enumerate(PAR["pairs"]):
            bank = "D%d" % (u % 2)
            for k in (2 * n, 2 * n + 1):
                a, cb = k // 3, k % 3
                mm([(ap(bank, s_[:, 193 * (k % 2):193 * (k % 2) + 193]), ap("Lm", s_[32 * a:32 * a + 32, 4 * cb:4 * cb + 4, :]),
                     ap("Rr", s_[32 * a:32 * a + 32, 0:193]))])
                ops[-1]["fence"] = k % 2 == 1 and cb == 0
            if ENG["D"][n] == "V":
                scan(ap("acc", s_[:, 386 * n:386 * n + 386]), ap("rsd"), ap(bank, s_[:, 0:386]), 0.0, A.add, A.max)
            for k in (2 * n, 2 * n + 1) if ENG["D"][n] == "S" else ():
                act(ap("junk", s_[:, 200 * (k % 2):200 * (k % 2) + 193]), ap(bank, s_[:, 193 * (k % 2):193 * (k % 2) + 193]), AF.Relu,
                    -45056.0, 1.0, ap("acc", s_[:, 193 * k + 192:193 * k + 193]))
        if "V" in ENG["D"]:
            tt(ap("flag"), ap("acc", s_[:, 192::193]), ap("TH"), A.is_gt)
        else:
            act(ap("flag"), ap("acc", s_[:, 192::193]), AF.Sign)
        Yb = ap("D0", s_[:, 400:412])
        for a in range(4):
            mm([(ap("D0", s_[32 * a:32 * a + 32, 400:412]), ap("Ib", s_[:, 32 * a:32 * a + 32]), ap("wf"))]
               + [(ap("D0", s_[32 * a:32 * a + 32, 400 + x:412:4]), ap("Fold", s_[:, 32 * x:32 * x + 32]),
                   ap("flag", s_[:, 3 * a:3 * a + 3])) for x in range(4)])
        tt(ap("off32"), Yb, ap("dum"), A.min)
        off = ap("off", s_[:, 0:12])
        copy(off, ap("off32"))
        if sent:
            remote(ap("RO%d" % st), ap("off"))
        if st < NST:
            copy(ind(ap(TB), off), ap("SRC"))
            lin(ENG["mf"], ap("mf"), dump)
        if sent:
            copy(ind(ap(NX), ap("RO%d" % st, s_[:, 0:12])), ap("RD%d" % st))
        if (ep, st - NEV * ep) == (0, PAR["ahead"][0]):
            ahead("TB1", "CM1", "RC1", "TB2")
        if st - NEV == PAR["ahead"][1]:
            ahead("TB2", "CM2", "RC2", "TB3")

    for st in range(1, NST + 1):
        tag[1] = st
        for part, cs in ((choose, (0, 1)), (winners, (2,)), (letters, (0, 1))):
            for c in cs:
                tag[0] = c
                part(st, c) if c < 2 else part(st)
    for k, o in enumerate((ap("yent", s_[:, 0:NW]), ap("yent", s_[:, NW:]), ap("yelen"))):
        dma(o, ap("TB3", s_[TROW[k]::16, 0:NW]))
    for e, names in PAR["first"].items():
        mine, last = [i for i, o in enumerate(ops) if o["eng"] == e and o["st"] == 0], None
        for nm in [x.split("*")[0] for x in names.split() for _ in range(int((x + "*1").split("*")[1]))]:
            if nm == "|":
                gate = last
                continue
            i = [i for i in mine if ops[i]["wr"][0][0] == nm][0]
            mine.remove(i)
            ops[i]["after"], last = last, i
        for i in mine:
            ops[i]["after"] = gate
    return ops


def link(ops):
    hist = {}
    for i, o in enumerate(ops):
        d = {}
        for mine, lst in ((False, o["rd"]), (True, o["wr"])):
            for bx in lst:
                for (j, w, b2) in hist.get(bx[0], []):
                    if (w or mine) and bx[2] <= b2[3] and b2[2] <= bx[3] and not bx[1].isdisjoint(b2[1]):
                        d[j] = d.get(j, False) or w
        o["dep"] = d
        o["banks"] = sorted(set((b[0], k) for b in o["rd"] + o["wr"] if b[0] in SCRATCH and SCRATCH[b[0]][0] == "psum"
                                for k in range(b[2] // 512, b[3] // 512 + 1)))
        for w, lst in ((False, set(o["rd"])), (True, set(o["wr"]))):
            for bx in lst:
                hist.setdefault(bx[0], []).append((i, w, bx))


def span(o):
    k, a = o["kind"], o["args"]
    size = {F32: 4, I32: 4, BF: 2, F16: 2, U16: 2}
    if k == "mm":
        t = sum(max(min(64, _box(l)[4]), _box(r)[4]) * (1.68 if _dt(l[0]) == F32 else 0.42) for (_, l, r, _, _) in a)
        return t, t + 100
    n = o["wr"][0][4]
    if k in ("dma", "rem"):
        by = n * len(o["wr"][0][1]) * size[_dt(a[1][0])]
        return (60, 1900 + by / 300, by / 300) if k == "dma" else (400, 2500 + by / 64, by / 128)
    if len(a[0]) == 3:
        t = 50 + 0.83 * 3 * _box(a[1])[4]
    elif isinstance(a[1], tuple) and len(a[1]) == 3:
        t = 60 + 0.83 * (max(2, PAR["ga"]) if k == "tt" else PAR["ga"]) * n
    elif o["eng"] == "G":
        t = 150 + 1.66 * n
    elif o["eng"] == "S":
        t = 65 + 0.83 * n + (20 if a[5] else 0)
    else:
        wide = [b for b in o["rd"] + o["wr"] if b[4] == n]
        psum = any(SCRATCH[b[0]][0] == "psum" for b in wide)
        rate = (1 if psum else 2) if k == "tt" else 0.5 if all(size[_dt(b[0])] == 2 for b in wide) else 1
        t = 30 + 0.83 * max(64, n * rate)
    return t, t


def schedule(ops):
    n, wake = len(ops), 60
    sp = [tuple(int(x) for x in span(o)) for o in ops]
    pred = [[(j, sp[j][0] if ops[j]["eng"] == "P" == o["eng"] and not o.get("fence") else sp[j][1] + (PAR["gwake"] if o["eng"] == "G" else wake))
             for j in o["dep"]] for o in ops]
    succ = [[] for _ in ops]
    for i, o in enumerate(ops):
        if o.get("after") is not None:
            pred[i].append((o["after"], sp[o["after"]][0]))
    topo, seen = [], set()

    def visit(i):
        if i not in seen:
            seen.add(i)
            for (j, lag) in pred[i]:
                visit(j)
            topo.append(i)
    for i in range(n):
        visit(i)
    for i in range(n):
        for (j, lag) in pred[i]:
            succ[j].append((i, lag))
    uses = [[(o["eng"], sp[i][0], None)] + [(b, sp[i][1] + wake, o["eng"]) for b in o["banks"]] for i, o in enumerate(ops)]

    def place(order, back):
        at, busy = [0] * n, {}
        for i in order:
            t = max([at[k] + lag for (k, lag) in succ[i]] + [sp[i][1]]) if back else max([at[j] + lag for (j, lag) in pred[i]], default=0)
            moved = True
            while moved:
                moved = False
                for (res, d, e) in uses[i]:
                    lo = t - d if back else t
                    lst = busy.get(res, ())
                    k = len(lst)
                    while k and lst[k - 1][0] > lo - 4000:
                        k -= 1
                    for (a, b, e2) in lst[k:]:
                        if a >= lo + d:
                            break
                        if lo < b and (e is None or e != e2):
                            t += b - lo
                            lo, moved = b, True
            at[i] = t
            for (res, d, e) in uses[i]:
                lst = busy.setdefault(res, [])
                lo = t - d if back else t
                k = len(lst)
                while k and lst[k - 1][0] > lo:
                    k -= 1
                lst.insert(k, (lo, lo + d, e))
        return at
    lead = [PAR["lead"].get(o["name"], 0) for o in ops]
    way = [0] * n
    for i in reversed(topo):
        way[i] = max([way[k] + lag for (k, lag) in succ[i]] + [sp[i][1]])
        if ops[i]["name"] in ("VMx0.0", "VMx1.0") and PAR["beat"]:
            beat, behind, tail = PAR["beat"]
            way[i] = max(way[i], tail + beat * (NST - ops[i]["st"]) + behind * (ops[i]["name"] == "VMx0.0"))
    best = None
    rng = np.random.default_rng(PAR.get("seed", 1))
    for _ in range(PAR["rounds"]):
        for i in reversed(topo):
            way[i] = max([way[k] + 1 for (k, lag) in succ[i]] + [way[i] + lead[i]])
        at = place(sorted(range(n), key=lambda i: (-way[i], i)), False)
        end = max(at[i] + sp[i][1] for i in range(n))
        if best is None or end <= best[0]:
            best = (end, at)
        rnd = [int(x) for x in rng.integers(0, PAR["noise"] + 1, n)]
        fin = [0] * n
        for i in topo:
            fin[i] = max([best[1][i] + sp[i][1] + rnd[i]] + [fin[j] + 1 for (j, lag) in pred[i]])
        way = place(sorted(range(n), key=lambda i: (-fin[i], -i)), True)
    return polish(ops, sp, sorted(topo, key=lambda i: best[1][i]))


def polish(ops, sp, order):
    n, wake = len(ops), 60
    engs = sorted(set(o["eng"] for o in ops))
    banks = sorted(set(b for o in ops for b in o["banks"]))
    eng = [engs.index(o["eng"]) for o in ops]
    bk = [[banks.index(b) for b in o["banks"]] for o in ops]
    dep = [list(o["dep"]) + ([] if o.get("after") is None else [o["after"]]) for o in ops]
    data = [[j for j in o["dep"] if not (ops[j]["eng"] == "P" == o["eng"] and not o.get("fence"))] for o in ops]
    deps = [set(d) for d in dep]
    wakes = [PAR["gwake"] if e == "G" else wake for e in engs]

    def run(order):
        done, why = [0] * n, [None] * n
        free, last, turn, dma = [0] * len(engs), [None] * len(engs), [{} for _ in banks], 0
        for i in order:
            e = eng[i]
            t, w = free[e], (last[e], True)
            wk = wakes[e]
            for j in data[i]:
                if done[j] + wk > t:
                    t, w = done[j] + wk, (j, False)
            for b in bk[i]:
                for e2, j in turn[b].items():
                    if e2 != e and done[j] + wake > t:
                        t, w = done[j] + wake, (j, j not in deps[i])
                turn[b][e] = i
            s = sp[i]
            free[e], last[e], why[i] = t + s[0], i, w
            if len(s) == 2:
                done[i] = t + s[1]
            else:
                if dma > t + s[0] + 900:
                    why[i] = (lastd, True)
                dma, lastd = max(dma, t + s[0] + 900) + s[2], i
                done[i] = dma + s[1] - s[2] - 900
        return max(done) + sum(done) * PAR["pull"] / n, done, why
    rng = np.random.default_rng(2)
    cur = run(order)
    best = (cur[0], order, max(cur[1]))
    for it in range(PAR["swaps"]):
        done, why = cur[1], cur[2]
        u = rng.random(6)
        i = done.index(max(done)) if u[0] < 0.5 else order[int(u[1] * n)]
        held = []
        while i is not None:
            j, res = why[i]
            if res and j is not None:
                held.append((j, i))
            i = j
        if not held:
            continue
        j, i = held[int(u[2] * len(held))]
        a, b = order.index(j), order.index(i)
        if u[4] < 0.5:
            if it % 2:
                a = max(0, a - int(u[5] * PAR["jump"]))
                j = order[a]
            else:
                b = min(n - 1, b + int(u[5] * PAR["jump"]))
                i = order[b]
        seg = order[a:b + 1]
        if it % 2:
            grp = {i}
            for x in reversed(seg[:-1]):
                if any(x in deps[y] for y in grp):
                    grp.add(x)
            new = [x for x in seg if x in grp] + [x for x in seg if x not in grp]
        else:
            grp = {j}
            for x in seg[1:]:
                if not deps[x].isdisjoint(grp):
                    grp.add(x)
            new = [x for x in seg if x not in grp] + [x for x in seg if x in grp]
        if i in grp and j in grp:
            continue
        cand = order[:a] + new + order[b + 1:]
        res = run(cand)
        heat = PAR["heat"] * (1 - it / PAR["swaps"])
        if res[0] <= cur[0] - heat * np.log(1 - u[3]):
            order, cur = cand, res
            if res[0] < best[0]:
                best = (res[0], cand, max(res[1]))
    PAR["est"] = best[2]
    return best[1]


def plan():
    ops = build()
    link(ops)
    order = schedule(ops)
    cnt, nd, nr, bank = {}, 0, 0, {}
    for i in order:
        o = ops[i]
        for b in o["banks"]:
            for e, j in bank.setdefault(b, {}).items():
                if e != o["eng"]:
                    o["dep"][j] = True
            bank[b][o["eng"]] = i
        if o["kind"] == "dma":
            o["sig"] = ("d%d" % nd, 16)
            nd += 1
        elif o["kind"] == "rem":
            o["sig"] = nr
            nr += 1
        else:
            cnt[o["eng"]] = cnt.get(o["eng"], 0) + 1
            o["sig"] = ("s" + o["eng"], cnt[o["eng"]])
    return ops, order, cnt, nd, nr


_PLAN = []


def rank_program(g, core, T, topo):
    rank = T.rank_of(core)
    if rank is None:
        return
    if not _PLAN:
        _PLAN.append(plan())
    ops, order, cnt, nd, nr = _PLAN[0]
    nxt = T.cores[(rank + 1) % len(T.cores)]
    prv = T.cores[(rank - 1) % len(T.cores)]
    rid, pid = topo.addr(nxt, core)
    mask = topo.mask(core, nxt)
    n_out, n_in = len(topo.engines(core, nxt)), len(topo.engines(prv, core))
    Q = {"V": g.vector, "S": g.scalar, "P": g.tensor, "G": g, "Y": g.sync}

    def r(x):
        if not isinstance(x, tuple):
            return x
        v = T[x[0]][x[1]]
        return v.indirect(r(x[2])) if len(x) == 3 else v

    seen = {}

    def wait(e, sem, val):
        if seen.get((e, sem), 0) < val:
            seen[(e, sem)] = val
            Q[e].wait_ge(T.sem[sem], val)

    for i in order:
        o = ops[i]
        e, k, a = o["eng"], o["kind"], o["args"]
        need = {}
        for j, w in o["dep"].items():
            p = ops[j]
            if p["kind"] == "rem":
                sem, val = ("r%d" % p["sig"], n_in) if w else ("l%d" % p["sig"], n_out)
            else:
                sem, val = p["sig"]
            if e == "P" and sem == "sP" and not o.get("fence"):
                continue
            need[sem] = max(need.get(sem, 0), val)
        for sem in sorted(need):
            wait(e, sem, need[sem])
        q = Q[e]
        if k == "rem":
            g.remote_dma(r(a[0]), r(a[1]), T.sem["r%d" % o["sig"]], T.sem["l%d" % o["sig"]], pid, rid, mask)
            continue
        if k == "copy":
            x = q.tensor_copy(r(a[0]), r(a[1]))
        elif k == "ts":
            x = (q.tensor_scalar(r(a[0]), r(a[1]), r(a[2]), None, a[4]) if a[5] is None
                 else q.tensor_scalar(r(a[0]), r(a[1]), r(a[2]), r(a[3]), a[4], a[5]))
        elif k == "tt":
            x = q.tensor_tensor(r(a[0]), r(a[1]), r(a[2]), a[3])
        elif k == "mset":
            x = q.memset(r(a[0]), a[1])
        elif k == "scan":
            x = q.tensor_tensor_scan(r(a[0]), r(a[1]), r(a[2]), a[3], a[4], a[5])
        elif k == "vtr":
            x = q.transpose(r(a[0]), r(a[1]))
        elif k == "act":
            if a[5] is None:
                x = q.activation(r(a[0]), r(a[1]), a[2], bias=r(a[3]), scale=r(a[4]))
            else:
                x = q.activation(r(a[0]), r(a[1]), a[2], bias=r(a[3]), scale=r(a[4]), accum_out=r(a[5]))
        elif k == "mm":
            for (out, l, rh, s0, s1) in a:
                x = q.matmul(r(out), r(l), r(rh), s0, s1)
        elif k == "iota":
            if _dt(a[0][0]) == I32:
                x = q.iota(r(a[0]), a[1], a[2], a[3])
            else:
                x = q.iota(r(a[0]), a[1], a[2], a[3], allow_small_or_imprecise_dtypes=True)
        elif k == "asel":
            x = q.affine_select(r(a[0]), r(a[1]), a[2], a[3], a[4], a[5], a[6])
        else:
            x = q.dma_start(r(a[0]), r(a[1]))
        x.then_inc(T.sem[o["sig"][0]], 16 if k == "dma" else 1)
    for e in sorted(cnt):
        wait("G", "s" + e, cnt[e])
    for k in range(nd):
        wait("G", "d%d" % k, 16)
    for k in range(nr):
        wait("G", "r%d" % k, n_in)
        wait("G", "l%d" % k, n_out)
